import numpy as np
import ml_dtypes


def mxq(x, axis, fmt="e4m3"):
    dtype, down = {"e4m3": (ml_dtypes.float8_e4m3fn, 7), "e5m2": (ml_dtypes.float8_e5m2, 14)}[fmt]
    v = np.moveaxis(np.asarray(x, np.float32).astype(ml_dtypes.bfloat16).astype(np.float64), axis, -1)
    blocks = v.reshape(v.shape[:-1] + (-1, 32))
    amax = np.abs(blocks).max(-1, keepdims=True)
    byte = np.maximum(np.where(amax > 0, np.frexp(amax)[1] - 1 + 127, 0) - down, 1)
    scale = np.exp2(byte - 127.0)
    codes = (blocks / scale).astype(np.float32).astype(dtype).astype(np.float64)
    return np.moveaxis((codes * scale).reshape(v.shape), -1, axis)


WIDE = False


def mx_kscale(k):
    if not WIDE:
        return np.ones(k)
    levels = np.array([10, -10, 5, -5, 0])
    if k % 512:
        return np.exp2(np.random.permutation(np.resize(levels, k // 32))).repeat(32)
    a = np.empty((k // 512, 16))
    for p in range(k // 512):
        a[p, :8] = np.random.permutation(np.resize(levels, 8))
        for g in range(8):
            far = levels[np.abs(levels - a[p, g]) >= 10]
            a[p, g + 8] = far[np.random.randint(len(far))]
    return np.exp2(a.ravel()).repeat(32)


def f64(x):
    return np.asarray(x).astype(np.float64)


def striped(idx):
    return np.tile(idx.reshape(-1, 16).T, (8, 1)).astype(np.uint16)


def unstriped(offs):
    return offs[:16].T.reshape(-1).astype(np.int64)


def pack_weight(w):
    k, n = w.shape
    w = f64(np.asarray(w, np.float32).astype(ml_dtypes.bfloat16)).reshape(k // 32, 32, n)
    amax = np.abs(w).max(1)
    byte = np.clip(np.where(amax > 0, np.frexp(amax)[1] - 1 + 127 - 7, 1), 1, 254)
    scaled = (w * np.exp2(127.0 - byte)[:, None, :]).reshape(k, n).astype(np.float32)
    words = np.ascontiguousarray(scaled.reshape(k // 512, 128, 4, n).transpose(0, 1, 3, 2)).astype(ml_dtypes.float8_e4m3fn).view(np.uint8)
    return words, np.ascontiguousarray(byte.astype(np.uint8).reshape(k // 512, 16, n))


def unpack_weight(words, scales):
    g, p, n, _ = words.shape
    vals = np.ascontiguousarray(words).view(ml_dtypes.float8_e4m3fn).astype(np.float64) * np.repeat(np.exp2(scales.astype(np.float64) - 127.0), 8, axis=1)[..., None]
    return vals.transpose(0, 1, 3, 2).reshape(g * 512, n)


def relu(v):
    return np.maximum(v, 0.0)


K, T, S, H, N, U = 1024, 2048, 512, 512, 256, 1024
P = 2 ** 7


def setup_inputs():
    n = np.random.standard_normal
    s = mx_kscale(K)[:, None]
    u = mx_kscale(H)
    packed_xT = pack_weight(n((K, T)) * s)
    return {
        "x_words": packed_xT[0],
        "x_scales": packed_xT[1],
        "mem": (n((H, U)) * u[:, None]).astype(np.float32),
        "gap": (np.tile(np.random.uniform(0.1, 2.0, S), (P, 1))).astype(np.float32),
        "rate": (0.7 * n((H, 1))).astype(np.float32),
        "off": (0.3 * n((H, 1))).astype(np.float32),
        "w1": (n((K, N)) / np.sqrt(2 * K) / s).astype(np.float32),
        "rr": (n((H, N)) / np.sqrt(2 * H) / u[:, None]).astype(np.float32),
        "offs": striped(np.random.permutation(T)[:S]),
        "slot": striped(np.random.permutation(U)[:S]),
    }


def reference(x_words, x_scales, mem, gap, rate, off, w1, rr, offs, slot):
    fade = np.exp(-1.0 * (relu(f64(rate) * f64(gap)[:1] + f64(off))))
    h = f64(mem)[:, unstriped(slot)] * fade
    xq = unpack_weight(x_words, x_scales)[:, unstriped(offs)]
    return np.tanh(mxq(f64(rr), 0, "e4m3").T @ mxq(h, 0, "e4m3") + mxq(f64(w1), 0, "e4m3").T @ xq)

@@ -1,0 +1,155 @@
+from contextlib import ExitStack
+
+import concourse.mybir as mybir
+
+K, T, S, H, N, U = 1024, 2048, 512, 512, 256, 1024
+FLOPS = 2 * (K + H) * N * S
+
+F32 = mybir.dt.float32
+BF16 = mybir.dt.bfloat16
+I32 = mybir.dt.int32
+U32 = mybir.dt.uint32
+U16 = mybir.dt.uint16
+U8 = mybir.dt.uint8
+FP8X4 = mybir.dt.float8_e4m3fn_x4
+ACT = mybir.ActivationFunctionType
+ALU = mybir.AluOpType
+
+P = 128
+PACK = 4
+HALF = S // 2
+
+
+def interleave(engine_copy, dst, src):
+    engine_copy(
+        out=dst.rearrange("p (c i) t -> p c t i", i=4),
+        in_=src.rearrange("p t (c i) -> p c t i", i=4),
+    )
+
+
+def tile_picked_ygrud_cand_p_kernel(
+    tc, x_words, x_scales, mem, gap, rate, off, w1, rr, offs, slot, out
+):
+    nc = tc.nc
+    with ExitStack() as ctx:
+        keep = ctx.enter_context(tc.tile_pool(name="keep", bufs=1))
+        psum = ctx.enter_context(tc.psum_pool(name="psum", bufs=1))
+
+        def sb(name, shape, dtype):
+            return keep.tile(shape, dtype, name=name, align_bytes=64)
+
+        offs_sb = sb("offs_sb", [P, S // 16], U16)
+        slot_sb = sb("slot_sb", [P, S // 16], U16)
+        gap_sb = sb("gap_sb", [P, S], F32)
+        rate_sb = sb("rate_sb", [P, PACK], F32)
+        off_sb = sb("off_sb", [P, PACK], F32)
+        mem_sb = [sb(f"mem{t}", [P, U], F32) for t in range(PACK)]
+        words_sb = [sb(f"words{g}", [P, T], U32) for g in range(2)]
+        scales_sb = sb("scales_sb", [P, T], U8)
+        w_raw = [sb(f"w_raw{g}", [P, PACK, N], F32) for g in range(3)]
+        w_src = [rr, w1[0:512, :], w1[512:1024, :]]
+
+        warm = sb("warm", [P, 1], F32)
+        warm_out = sb("warm_out", [P, 1], F32)
+        nc.vector.memset(warm[:], 0.0)
+        nc.vector.memset(scales_sb[:].bitcast(I32), 0)
+
+        mem_rows = mem.rearrange("(p t) u -> t p u", t=PACK)
+        nc.scalar.activation(out=warm_out[:], in_=warm[:], func=ACT.Exp)
+
+        def load_w(g):
+            nc.sync.dma_start(out=w_raw[g][:], in_=w_src[g].rearrange("(p t) n -> p t n", t=PACK))
+
+        nc.sync.dma_start(out=gap_sb[:], in_=gap)
+        nc.sync.dma_start(out=rate_sb[:], in_=rate.rearrange("(p t) o -> p (t o)", t=PACK))
+        nc.sync.dma_start(out=off_sb[:], in_=off.rearrange("(p t) o -> p (t o)", t=PACK))
+        nc.sync.dma_start(slot_sb[:], slot)
+        for t in range(PACK):
+            nc.sync.dma_start(out=mem_sb[t][:], in_=mem_rows[t])
+        nc.sync.dma_start(offs_sb[:], offs)
+        for g in range(3):
+            load_w(g)
+        for g in range(2):
+            nc.sync.dma_start(
+                out=words_sb[g][:].bitcast(I32),
+                in_=x_words[g].rearrange("p n t -> p (n t)").bitcast(I32),
+            )
+        for q in range(4):
+            nc.gpsimd.dma_start(
+                out=scales_sb[32 * q : 32 * q + 8, :].bitcast(I32),
+                in_=x_scales[:, 4 * q : 4 * q + 4, :].bitcast(I32),
+            )
+
+        neg_off = sb("neg_off", [P, PACK], F32)
+        nc.vector.tensor_scalar(neg_off[:], off_sb[:], -1.0, None, ALU.mult)
+        h32 = sb("h32", [P, PACK, S], F32)
+        fade = [sb(f"fade{t}", [P, S], F32) for t in range(PACK)]
+        for t in range(PACK):
+            decay = sb(f"decay{t}", [P, S], F32)
+            nc.vector.tensor_scalar(
+                decay[:], gap_sb[:], rate_sb[:, t : t + 1], neg_off[:, t : t + 1], ALU.mult, ALU.max
+            )
+            nc.scalar.activation(out=fade[t][:], in_=decay[:], func=ACT.Exp, scale=-1.0, bias=neg_off[:, t : t + 1])
+        for t in range(PACK):
+            nc.vector.tensor_tensor(h32[:, t, :], mem_sb[t][:].indirect(slot_sb[:]), fade[t][:], ALU.mult)
+
+        x_sc = keep.tile([P, S], U8, name="x_sc", tag="fade3", align_bytes=64)
+        nc.vector.tensor_copy(x_sc[:], scales_sb[:].indirect(offs_sb[:]))
+
+        w_codes = [sb(f"w_codes{g}", [P, N], U32) for g in range(3)]
+        w_sc = [sb(f"w_sc{g}", [P, N], U8) for g in range(3)]
+
+        def quant_w(g):
+            grouped = sb(f"w_bf{g}", [P, N, PACK], BF16)
+            interleave(nc.scalar.copy, grouped[:], w_raw[g][:])
+            nc.vector.quantize_mx(
+                out=w_codes[g][:].bitcast(FP8X4), scales=w_sc[g][:],
+                in_=grouped[:].rearrange("p n t -> p (n t)"),
+            )
+
+        h_codes = [sb(f"h_codes{b}", [P, HALF], U32) for b in range(2)]
+        h_sc = [sb(f"h_sc{b}", [P, HALF], U8) for b in range(2)]
+
+        def quant_h(b):
+            grouped = sb(f"h_bf{b}", [P, HALF, PACK], BF16)
+            interleave(nc.scalar.copy, grouped[:], h32[:, :, b * HALF : (b + 1) * HALF])
+            nc.vector.quantize_mx(
+                out=h_codes[b][:].bitcast(FP8X4), scales=h_sc[b][:],
+                in_=grouped[:].rearrange("p n t -> p (n t)"),
+            )
+
+        quant_w(0)
+        quant_w(1)
+        quant_h(0)
+        quant_h(1)
+        quant_w(2)
+
+        x0 = sb("x0", [P, S], U32)
+        nc.vector.tensor_copy(x0[:], words_sb[0][:].indirect(offs_sb[:]))
+        x1 = [sb(f"x1_{b}", [P, HALF], U32) for b in range(2)]
+        for b in range(2):
+            nc.vector.tensor_copy(x1[b][:], words_sb[1][:].indirect(offs_sb[:, 16 * b : 16 * (b + 1)]))
+
+        acc = [[psum.tile([P, HALF], F32, name=f"acc{b}{m}") for m in range(2)] for b in range(2)]
+
+        def mm(b, m, g, rhs, rhs_scale):
+            cols = slice(m * P, (m + 1) * P)
+            nc.tensor.matmul_mx(
+                out=acc[b][m][:], lhsT=w_codes[g][:, cols].bitcast(FP8X4), lhsT_scale=w_sc[g][:, cols],
+                rhs=rhs.bitcast(FP8X4), rhs_scale=rhs_scale, start=(g == 0), stop=(g == 2),
+            )
+
+        for b in range(2):
+            for m in range(2):
+                mm(b, m, 0, h_codes[b][:], h_sc[b][:])
+        for b in range(2):
+            js = slice(b * HALF, (b + 1) * HALF)
+            for m in range(2):
+                mm(b, m, 1, x0[:, js], x_sc[:, js])
+        for b in range(2):
+            js = slice(b * HALF, (b + 1) * HALF)
+            for m in range(2):
+                mm(b, m, 2, x1[b][:], x_sc[4:P, js])
+                res = sb(f"res{b}{m}", [P, HALF], F32)
+                nc.scalar.activation(out=res[:], in_=acc[b][m][:], func=ACT.Tanh)
+                nc.sync.dma_start(out=out[m * P : (m + 1) * P, js], in_=res[:])

@@ -35,8 +35,8 @@ def tile_picked_ygrud_cand_p_kernel(
         keep = ctx.enter_context(tc.tile_pool(name="keep", bufs=1))
         psum = ctx.enter_context(tc.psum_pool(name="psum", bufs=1))
 
-        def sb(name, shape, dtype):
-            return keep.tile(shape, dtype, name=name, align_bytes=64)
+        def sb(name, shape, dtype, tag=None):
+            return keep.tile(shape, dtype, name=name, tag=tag or name, align_bytes=64)
 
         offs_sb = sb("offs_sb", [P, S // 16], U16)
         slot_sb = sb("slot_sb", [P, S // 16], U16)
@@ -64,20 +64,30 @@ def tile_picked_ygrud_cand_p_kernel(
         nc.sync.dma_start(out=rate_sb[:], in_=rate.rearrange("(p t) o -> p (t o)", t=PACK))
         nc.sync.dma_start(out=off_sb[:], in_=off.rearrange("(p t) o -> p (t o)", t=PACK))
         nc.sync.dma_start(slot_sb[:], slot)
-        for t in range(PACK):
+
+        def load_scales(i):
+            g, q = divmod(i, 4)
+            nc.sync.dma_start(
+                out=scales_sb[32 * q + 4 * g : 32 * q + 4 * g + 4, :].bitcast(I32),
+                in_=x_scales[g, 4 * q : 4 * q + 4, :].bitcast(I32),
+            )
+
+        for t in range(PACK - 1):
             nc.sync.dma_start(out=mem_sb[t][:], in_=mem_rows[t])
+        load_w(0)
+        nc.sync.dma_start(out=mem_sb[3][:], in_=mem_rows[3])
         nc.sync.dma_start(offs_sb[:], offs)
-        for g in range(3):
-            load_w(g)
+        for i in (0, 1, 2):
+            load_scales(i)
+        load_w(1)
+        load_scales(3)
+        load_w(2)
+        for i in (4, 5, 6, 7):
+            load_scales(i)
         for g in range(2):
             nc.sync.dma_start(
                 out=words_sb[g][:].bitcast(I32),
                 in_=x_words[g].rearrange("p n t -> p (n t)").bitcast(I32),
-            )
-        for q in range(4):
-            nc.gpsimd.dma_start(
-                out=scales_sb[32 * q : 32 * q + 8, :].bitcast(I32),
-                in_=x_scales[:, 4 * q : 4 * q + 4, :].bitcast(I32),
             )
 
         neg_off = sb("neg_off", [P, PACK], F32)
@@ -93,14 +103,11 @@ def tile_picked_ygrud_cand_p_kernel(
         for t in range(PACK):
             nc.vector.tensor_tensor(h32[:, t, :], mem_sb[t][:].indirect(slot_sb[:]), fade[t][:], ALU.mult)
 
-        x_sc = keep.tile([P, S], U8, name="x_sc", tag="fade3", align_bytes=64)
-        nc.vector.tensor_copy(x_sc[:], scales_sb[:].indirect(offs_sb[:]))
-
-        w_codes = [sb(f"w_codes{g}", [P, N], U32) for g in range(3)]
+        w_codes = [sb(f"w_codes{g}", [P, N], U32, tag=tag) for g, tag in enumerate(("mem3", "fade3", "words0"))]
         w_sc = [sb(f"w_sc{g}", [P, N], U8) for g in range(3)]
 
-        def quant_w(g):
-            grouped = sb(f"w_bf{g}", [P, N, PACK], BF16)
+        def quant_w(g, tag):
+            grouped = sb(f"w_bf{g}", [P, N, PACK], BF16, tag=tag)
             interleave(nc.scalar.copy, grouped[:], w_raw[g][:])
             nc.vector.quantize_mx(
                 out=w_codes[g][:].bitcast(FP8X4), scales=w_sc[g][:],
@@ -110,25 +117,23 @@ def tile_picked_ygrud_cand_p_kernel(
         h_codes = [sb(f"h_codes{b}", [P, HALF], U32) for b in range(2)]
         h_sc = [sb(f"h_sc{b}", [P, HALF], U8) for b in range(2)]
 
-        def quant_h(b):
-            grouped = sb(f"h_bf{b}", [P, HALF, PACK], BF16)
-            interleave(nc.scalar.copy, grouped[:], h32[:, :, b * HALF : (b + 1) * HALF])
-            nc.vector.quantize_mx(
-                out=h_codes[b][:].bitcast(FP8X4), scales=h_sc[b][:],
-                in_=grouped[:].rearrange("p n t -> p (n t)"),
-            )
-
-        quant_w(0)
-        quant_w(1)
-        quant_h(0)
-        quant_h(1)
-        quant_w(2)
-
-        x0 = sb("x0", [P, S], U32)
-        nc.vector.tensor_copy(x0[:], words_sb[0][:].indirect(offs_sb[:]))
-        x1 = [sb(f"x1_{b}", [P, HALF], U32) for b in range(2)]
+        quant_w(0, None)
+        quant_w(1, None)
+        x_sc = sb("x_sc", [P, S], U8, tag="w_bf1")
+        nc.vector.tensor_copy(x_sc[:], scales_sb[:].indirect(offs_sb[:]))
+        h_bf = sb("h_bf", [P, S * PACK], BF16, tag="w_raw1")
         for b in range(2):
-            nc.vector.tensor_copy(x1[b][:], words_sb[1][:].indirect(offs_sb[:, 16 * b : 16 * (b + 1)]))
+            grouped = h_bf[:, b * HALF * PACK : (b + 1) * HALF * PACK]
+            interleave(nc.scalar.copy, grouped.rearrange("p (n t) -> p n t", t=PACK), h32[:, :, b * HALF : (b + 1) * HALF])
+            nc.vector.quantize_mx(out=h_codes[b][:].bitcast(FP8X4), scales=h_sc[b][:], in_=grouped)
+        x0 = sb("x0", [P, S], U32, tag="w_raw1")
+        nc.vector.tensor_copy(x0[:], words_sb[0][:].indirect(offs_sb[:]))
+        quant_w(2, "h32")
+        x1 = sb("x1", [P, S], U32, tag="h32")
+        for b in range(2):
+            nc.vector.tensor_copy(
+                x1[:, b * HALF : (b + 1) * HALF], words_sb[1][:].indirect(offs_sb[:, 16 * b : 16 * (b + 1)])
+            )
 
         acc = [[psum.tile([P, HALF], F32, name=f"acc{b}{m}") for m in range(2)] for b in range(2)]
 
@@ -149,7 +154,7 @@ def tile_picked_ygrud_cand_p_kernel(
         for b in range(2):
             js = slice(b * HALF, (b + 1) * HALF)
             for m in range(2):
-                mm(b, m, 2, x1[b][:], x_sc[4:P, js])
+                mm(b, m, 2, x1[:, js], x_sc[4:P, js])
                 res = sb(f"res{b}{m}", [P, HALF], F32)
                 nc.scalar.activation(out=res[:], in_=acc[b][m][:], func=ACT.Tanh)
                 nc.sync.dma_start(out=out[m * P : (m + 1) * P, js], in_=res[:])

@@ -1,6 +1,7 @@
 from contextlib import ExitStack
 
 import concourse.mybir as mybir
+from concourse.masks import make_identity
 
 K, T, S, H, N, U = 1024, 2048, 512, 512, 256, 1024
 FLOPS = 2 * (K + H) * N * S
@@ -20,13 +21,6 @@ PACK = 4
 HALF = S // 2
 
 
-def interleave(engine_copy, dst, src):
-    engine_copy(
-        out=dst.rearrange("p (c i) t -> p c t i", i=4),
-        in_=src.rearrange("p t (c i) -> p c t i", i=4),
-    )
-
-
 def tile_picked_ygrud_cand_p_kernel(
     tc, x_words, x_scales, mem, gap, rate, off, w1, rr, offs, slot, out
 ):
@@ -38,9 +32,15 @@ def tile_picked_ygrud_cand_p_kernel(
         def sb(name, shape, dtype, tag=None):
             return keep.tile(shape, dtype, name=name, tag=tag or name, align_bytes=64)
 
+        def interleave(copy, dst, src):
+            copy(
+                out=dst.rearrange("p (c i t) -> p c t i", i=4, t=PACK),
+                in_=src.rearrange("p t (c i) -> p c t i", i=4),
+            )
+
         offs_sb = sb("offs_sb", [P, S // 16], U16)
         slot_sb = sb("slot_sb", [P, S // 16], U16)
-        gap_sb = sb("gap_sb", [P, S], F32)
+        gap_col = sb("gap_col", [P, PACK], F32)
         rate_sb = sb("rate_sb", [P, PACK], F32)
         off_sb = sb("off_sb", [P, PACK], F32)
         mem_sb = [sb(f"mem{t}", [P, U], F32) for t in range(PACK)]
@@ -52,109 +52,106 @@ def tile_picked_ygrud_cand_p_kernel(
         warm = sb("warm", [P, 1], F32)
         warm_out = sb("warm_out", [P, 1], F32)
         nc.vector.memset(warm[:], 0.0)
+        nc.scalar.activation(out=warm_out[:], in_=warm[:], func=ACT.Exp)
         nc.vector.memset(scales_sb[:].bitcast(I32), 0)
+        ident = sb("ident", [P, P], F32)
+        make_identity(nc, ident[:])
 
         mem_rows = mem.rearrange("(p t) u -> t p u", t=PACK)
-        nc.scalar.activation(out=warm_out[:], in_=warm[:], func=ACT.Exp)
 
         def load_w(g):
             nc.sync.dma_start(out=w_raw[g][:], in_=w_src[g].rearrange("(p t) n -> p t n", t=PACK))
 
-        nc.sync.dma_start(out=gap_sb[:], in_=gap)
+        nc.sync.dma_start(out=gap_col[:], in_=gap[0].rearrange("(p c) -> p c", c=PACK))
         nc.sync.dma_start(out=rate_sb[:], in_=rate.rearrange("(p t) o -> p (t o)", t=PACK))
         nc.sync.dma_start(out=off_sb[:], in_=off.rearrange("(p t) o -> p (t o)", t=PACK))
         nc.sync.dma_start(slot_sb[:], slot)
-
-        def load_scales(i):
-            g, q = divmod(i, 4)
-            nc.sync.dma_start(
-                out=scales_sb[32 * q + 4 * g : 32 * q + 4 * g + 4, :].bitcast(I32),
-                in_=x_scales[g, 4 * q : 4 * q + 4, :].bitcast(I32),
-            )
-
-        for t in range(PACK - 1):
+        for t in range(PACK):
             nc.sync.dma_start(out=mem_sb[t][:], in_=mem_rows[t])
-        load_w(0)
-        nc.sync.dma_start(out=mem_sb[3][:], in_=mem_rows[3])
         nc.sync.dma_start(offs_sb[:], offs)
-        for i in (0, 1, 2):
-            load_scales(i)
-        load_w(1)
-        load_scales(3)
-        load_w(2)
-        for i in (4, 5, 6, 7):
-            load_scales(i)
+        for g in range(3):
+            load_w(g)
+        for q in range(4):
+            nc.gpsimd.dma_start(
+                out=scales_sb[32 * q : 32 * q + 8, :].bitcast(I32),
+                in_=x_scales[:, 4 * q : 4 * q + 4, :].bitcast(I32),
+            )
         for g in range(2):
             nc.sync.dma_start(
                 out=words_sb[g][:].bitcast(I32),
                 in_=x_words[g].rearrange("p n t -> p (n t)").bitcast(I32),
             )
 
+        gap_ps = psum.tile([P, PACK, P], F32, name="gap_ps")
+        for c in range(PACK):
+            nc.tensor.transpose(gap_ps[:, c, :], gap_col[:, c : c + 1].to_broadcast([P, P]), ident[:])
+
         neg_off = sb("neg_off", [P, PACK], F32)
         nc.vector.tensor_scalar(neg_off[:], off_sb[:], -1.0, None, ALU.mult)
+        gap_all = gap_ps[:].rearrange("m c p -> m p c")
         h32 = sb("h32", [P, PACK, S], F32)
         fade = [sb(f"fade{t}", [P, S], F32) for t in range(PACK)]
         for t in range(PACK):
             decay = sb(f"decay{t}", [P, S], F32)
-            nc.vector.tensor_scalar(
-                decay[:], gap_sb[:], rate_sb[:, t : t + 1], neg_off[:, t : t + 1], ALU.mult, ALU.max
-            )
-            nc.scalar.activation(out=fade[t][:], in_=decay[:], func=ACT.Exp, scale=-1.0, bias=neg_off[:, t : t + 1])
+            decay_pc = decay[:].rearrange("m (p c) -> m p c", c=PACK)
+            rate_t = rate_sb[:, t : t + 1]
+            if t < 2:
+                nc.vector.tensor_scalar(decay_pc, gap_all, rate_t, neg_off[:, t : t + 1], ALU.mult, ALU.max)
+                nc.scalar.activation(out=fade[t][:], in_=decay[:], func=ACT.Exp, scale=-1.0, bias=neg_off[:, t : t + 1])
+            else:
+                nc.scalar.activation(out=decay_pc, in_=gap_all, func=ACT.Relu, scale=rate_t, bias=off_sb[:, t : t + 1])
+                nc.scalar.activation(out=fade[t][:], in_=decay[:], func=ACT.Exp, scale=-1.0)
         for t in range(PACK):
             nc.vector.tensor_tensor(h32[:, t, :], mem_sb[t][:].indirect(slot_sb[:]), fade[t][:], ALU.mult)
 
-        w_codes = [sb(f"w_codes{g}", [P, N], U32, tag=tag) for g, tag in enumerate(("mem3", "fade3", "words0"))]
+        halves = [slice(b * HALF, (b + 1) * HALF) for b in range(2)]
+        offs_half = [offs_sb[:, 16 * b : 16 * (b + 1)] for b in range(2)]
+
+        w_codes = [sb(f"w_codes{g}", [P, N], U32) for g in range(3)]
         w_sc = [sb(f"w_sc{g}", [P, N], U8) for g in range(3)]
+        w_bf = [sb(f"w_bf{g}", [P, N * PACK], BF16) for g in range(3)]
+        h_codes = sb("h_codes", [P, S], U32)
+        h_sc = sb("h_sc", [P, S], U8)
 
-        def quant_w(g, tag):
-            grouped = sb(f"w_bf{g}", [P, N, PACK], BF16, tag=tag)
-            interleave(nc.scalar.copy, grouped[:], w_raw[g][:])
-            nc.vector.quantize_mx(
-                out=w_codes[g][:].bitcast(FP8X4), scales=w_sc[g][:],
-                in_=grouped[:].rearrange("p n t -> p (n t)"),
-            )
+        def quant_w(g):
+            nc.vector.quantize_mx(out=w_codes[g][:].bitcast(FP8X4), scales=w_sc[g][:], in_=w_bf[g][:])
 
-        h_codes = [sb(f"h_codes{b}", [P, HALF], U32) for b in range(2)]
-        h_sc = [sb(f"h_sc{b}", [P, HALF], U8) for b in range(2)]
+        def quant_h(b, grouped):
+            nc.vector.quantize_mx(out=h_codes[:, halves[b]].bitcast(FP8X4), scales=h_sc[:, halves[b]], in_=grouped[:])
 
-        quant_w(0, None)
-        quant_w(1, None)
-        x_sc = sb("x_sc", [P, S], U8, tag="w_bf1")
+        interleave(nc.scalar.copy, w_bf[0][:], w_raw[0][:])
+        interleave(nc.scalar.copy, w_bf[1][:], w_raw[1][:])
+        h_bf0 = sb("h_bf0", [P, HALF * PACK], BF16)
+        h_bf1 = sb("h_bf1", [P, HALF * PACK], BF16, tag="w_raw1")
+        interleave(nc.vector.tensor_copy, h_bf0[:], h32[:, :, halves[0]])
+        interleave(nc.scalar.copy, h_bf1[:], h32[:, :, halves[1]])
+        interleave(nc.scalar.copy, w_bf[2][:], w_raw[2][:])
+
+        x_sc = sb("x_sc", [P, S], U8, tag="fade3")
         nc.vector.tensor_copy(x_sc[:], scales_sb[:].indirect(offs_sb[:]))
-        h_bf = sb("h_bf", [P, S * PACK], BF16, tag="w_raw1")
-        for b in range(2):
-            grouped = h_bf[:, b * HALF * PACK : (b + 1) * HALF * PACK]
-            interleave(nc.scalar.copy, grouped.rearrange("p (n t) -> p n t", t=PACK), h32[:, :, b * HALF : (b + 1) * HALF])
-            nc.vector.quantize_mx(out=h_codes[b][:].bitcast(FP8X4), scales=h_sc[b][:], in_=grouped)
-        x0 = sb("x0", [P, S], U32, tag="w_raw1")
-        nc.vector.tensor_copy(x0[:], words_sb[0][:].indirect(offs_sb[:]))
-        quant_w(2, "h32")
-        x1 = sb("x1", [P, S], U32, tag="h32")
-        for b in range(2):
-            nc.vector.tensor_copy(
-                x1[:, b * HALF : (b + 1) * HALF], words_sb[1][:].indirect(offs_sb[:, 16 * b : 16 * (b + 1)])
-            )
+        quant_h(0, h_bf0)
+        quant_w(0)
+        quant_w(1)
+        quant_h(1, h_bf1)
+        quant_w(2)
+        x_codes = [sb(f"x_codes{g}", [P, S], U32) for g in range(2)]
+        for g in range(2):
+            for b in range(2):
+                nc.vector.tensor_copy(x_codes[g][:, halves[b]], words_sb[g][:].indirect(offs_half[b]))
+        x0, x1 = x_codes
 
         acc = [[psum.tile([P, HALF], F32, name=f"acc{b}{m}") for m in range(2)] for b in range(2)]
-
-        def mm(b, m, g, rhs, rhs_scale):
-            cols = slice(m * P, (m + 1) * P)
-            nc.tensor.matmul_mx(
-                out=acc[b][m][:], lhsT=w_codes[g][:, cols].bitcast(FP8X4), lhsT_scale=w_sc[g][:, cols],
-                rhs=rhs.bitcast(FP8X4), rhs_scale=rhs_scale, start=(g == 0), stop=(g == 2),
-            )
-
-        for b in range(2):
-            for m in range(2):
-                mm(b, m, 0, h_codes[b][:], h_sc[b][:])
-        for b in range(2):
-            js = slice(b * HALF, (b + 1) * HALF)
-            for m in range(2):
-                mm(b, m, 1, x0[:, js], x_sc[:, js])
-        for b in range(2):
-            js = slice(b * HALF, (b + 1) * HALF)
-            for m in range(2):
-                mm(b, m, 2, x1[:, js], x_sc[4:P, js])
-                res = sb(f"res{b}{m}", [P, HALF], F32)
-                nc.scalar.activation(out=res[:], in_=acc[b][m][:], func=ACT.Tanh)
-                nc.sync.dma_start(out=out[m * P : (m + 1) * P, js], in_=res[:])
+        moving = [(h_codes, h_sc, 0), (x0, x_sc, 0), (x1, x_sc, 4)]
+        for g, (codes, scales, row0) in enumerate(moving):
+            for b in range(2):
+                for m in range(2):
+                    cols = slice(m * P, (m + 1) * P)
+                    nc.tensor.matmul_mx(
+                        out=acc[b][m][:], lhsT=w_codes[g][:, cols].bitcast(FP8X4), lhsT_scale=w_sc[g][:, cols],
+                        rhs=codes[:, halves[b]].bitcast(FP8X4), rhs_scale=scales[row0:P, halves[b]],
+                        start=(g == 0), stop=(g == 2),
+                    )
+                    if g == 2:
+                        res = sb(f"res{b}{m}", [P, HALF], F32)
+                        nc.scalar.activation(out=res[:], in_=acc[b][m][:], func=ACT.Tanh)
+                        nc.sync.dma_start(out=out[cols, halves[b]], in_=res[:])

@@ -49,10 +49,6 @@ def tile_picked_ygrud_cand_p_kernel(
         w_raw = [sb(f"w_raw{g}", [P, PACK, N], F32) for g in range(3)]
         w_src = [rr, w1[0:512, :], w1[512:1024, :]]
 
-        warm = sb("warm", [P, 1], F32)
-        warm_out = sb("warm_out", [P, 1], F32)
-        nc.vector.memset(warm[:], 0.0)
-        nc.scalar.activation(out=warm_out[:], in_=warm[:], func=ACT.Exp)
         nc.vector.memset(scales_sb[:].bitcast(I32), 0)
         ident = sb("ident", [P, P], F32)
         make_identity(nc, ident[:])
@@ -69,9 +65,19 @@ def tile_picked_ygrud_cand_p_kernel(
         for t in range(PACK):
             nc.sync.dma_start(out=mem_sb[t][:], in_=mem_rows[t])
         nc.sync.dma_start(offs_sb[:], offs)
+
+        def load_scales(g, q):
+            nc.sync.dma_start(
+                out=scales_sb[32 * q + 4 * g : 32 * q + 4 * g + 4, :].bitcast(I32),
+                in_=x_scales[g, 4 * q : 4 * q + 4, :].bitcast(I32),
+            )
+
         for g in range(3):
             load_w(g)
-        for q in range(4):
+            if g < 2:
+                for q in (2, 3):
+                    load_scales(g, q)
+        for q in range(2):
             nc.gpsimd.dma_start(
                 out=scales_sb[32 * q : 32 * q + 8, :].bitcast(I32),
                 in_=x_scales[:, 4 * q : 4 * q + 4, :].bitcast(I32),

@@ -58,11 +58,12 @@ def tile_picked_ygrud_cand_p_kernel(
         def load_w(g):
             nc.sync.dma_start(out=w_raw[g][:], in_=w_src[g].rearrange("(p t) n -> p t n", t=PACK))
 
+        nc.sync.dma_start(slot_sb[:], slot)
+        nc.sync.dma_start(out=mem_sb[0][:], in_=mem_rows[0])
         nc.sync.dma_start(out=gap_col[:], in_=gap[0].rearrange("(p c) -> p c", c=PACK))
         nc.sync.dma_start(out=rate_sb[:], in_=rate.rearrange("(p t) o -> p (t o)", t=PACK))
         nc.sync.dma_start(out=off_sb[:], in_=off.rearrange("(p t) o -> p (t o)", t=PACK))
-        nc.sync.dma_start(slot_sb[:], slot)
-        for t in range(PACK):
+        for t in range(1, PACK):
             nc.sync.dma_start(out=mem_sb[t][:], in_=mem_rows[t])
         nc.sync.dma_start(offs_sb[:], offs)
 
@@ -92,54 +93,46 @@ def tile_picked_ygrud_cand_p_kernel(
         for c in range(PACK):
             nc.tensor.transpose(gap_ps[:, c, :], gap_col[:, c : c + 1].to_broadcast([P, P]), ident[:])
 
-        neg_off = sb("neg_off", [P, PACK], F32)
-        nc.vector.tensor_scalar(neg_off[:], off_sb[:], -1.0, None, ALU.mult)
-        gap_all = gap_ps[:].rearrange("m c p -> m p c")
-        h32 = sb("h32", [P, PACK, S], F32)
-        fade = [sb(f"fade{t}", [P, S], F32) for t in range(PACK)]
-        for t in range(PACK):
-            decay = sb(f"decay{t}", [P, S], F32)
-            decay_pc = decay[:].rearrange("m (p c) -> m p c", c=PACK)
-            rate_t = rate_sb[:, t : t + 1]
-            if t < 2:
-                nc.vector.tensor_scalar(decay_pc, gap_all, rate_t, neg_off[:, t : t + 1], ALU.mult, ALU.max)
-                nc.scalar.activation(out=fade[t][:], in_=decay[:], func=ACT.Exp, scale=-1.0, bias=neg_off[:, t : t + 1])
-            else:
-                nc.scalar.activation(out=decay_pc, in_=gap_all, func=ACT.Relu, scale=rate_t, bias=off_sb[:, t : t + 1])
-                nc.scalar.activation(out=fade[t][:], in_=decay[:], func=ACT.Exp, scale=-1.0)
-        for t in range(PACK):
-            nc.vector.tensor_tensor(h32[:, t, :], mem_sb[t][:].indirect(slot_sb[:]), fade[t][:], ALU.mult)
-
         halves = [slice(b * HALF, (b + 1) * HALF) for b in range(2)]
         offs_half = [offs_sb[:, 16 * b : 16 * (b + 1)] for b in range(2)]
 
-        w_codes = [sb(f"w_codes{g}", [P, N], U32) for g in range(3)]
-        w_sc = [sb(f"w_sc{g}", [P, N], U8) for g in range(3)]
-        w_bf = [sb(f"w_bf{g}", [P, N * PACK], BF16) for g in range(3)]
+        picked = sb("picked", [P, PACK, S], F32)
+        for t in range(PACK):
+            nc.vector.tensor_copy(picked[:, t, :], mem_sb[t][:].indirect(slot_sb[:]))
+
         h_codes = sb("h_codes", [P, S], U32)
         h_sc = sb("h_sc", [P, S], U8)
+        h_bf = []
+        for b in range(2):
+            decay = sb(f"decay{b}", [P, PACK, HALF], F32)
+            fade = sb(f"fade{b}", [P, PACK, HALF], F32)
+            gap_half = gap_ps[:, :, b * P // 2 : (b + 1) * P // 2].rearrange("m c p -> m p c")
+            for t in range(PACK):
+                nc.scalar.activation(
+                    out=decay[:, t, :].rearrange("m (p c) -> m p c", c=PACK), in_=gap_half,
+                    func=ACT.Relu, scale=rate_sb[:, t : t + 1], bias=off_sb[:, t : t + 1],
+                )
+            nc.scalar.activation(out=fade[:], in_=decay[:], func=ACT.Exp, scale=-1.0)
+            h_bf.append(sb(f"h_bf{b}", [P, HALF * PACK], BF16))
+            nc.vector.tensor_tensor(
+                h_bf[b][:].rearrange("p (c i t) -> p c t i", i=4, t=PACK),
+                picked[:, :, halves[b]].rearrange("p t (c i) -> p c t i", i=4),
+                fade[:].rearrange("p t (c i) -> p c t i", i=4),
+                ALU.mult,
+            )
+        for b in range(2):
+            nc.vector.quantize_mx(out=h_codes[:, halves[b]].bitcast(FP8X4), scales=h_sc[:, halves[b]], in_=h_bf[b][:])
 
-        def quant_w(g):
-            nc.vector.quantize_mx(out=w_codes[g][:].bitcast(FP8X4), scales=w_sc[g][:], in_=w_bf[g][:])
+        x_sc = sb("x_sc", [P, S], U8)
+        w_codes = [sb(f"w_codes{g}", [P, N], U32) for g in range(3)]
+        w_sc = [sb(f"w_sc{g}", [P, N], U8) for g in range(3)]
+        for g in range(3):
+            w_bf = sb(f"w_bf{g}", [P, N * PACK], BF16)
+            interleave(nc.scalar.copy, w_bf[:], w_raw[g][:])
+            nc.vector.quantize_mx(out=w_codes[g][:].bitcast(FP8X4), scales=w_sc[g][:], in_=w_bf[:])
+            if g == 0:
+                nc.vector.tensor_copy(x_sc[:], scales_sb[:].indirect(offs_sb[:]))
 
-        def quant_h(b, grouped):
-            nc.vector.quantize_mx(out=h_codes[:, halves[b]].bitcast(FP8X4), scales=h_sc[:, halves[b]], in_=grouped[:])
-
-        interleave(nc.scalar.copy, w_bf[0][:], w_raw[0][:])
-        interleave(nc.scalar.copy, w_bf[1][:], w_raw[1][:])
-        h_bf0 = sb("h_bf0", [P, HALF * PACK], BF16)
-        h_bf1 = sb("h_bf1", [P, HALF * PACK], BF16, tag="w_raw1")
-        interleave(nc.vector.tensor_copy, h_bf0[:], h32[:, :, halves[0]])
-        interleave(nc.scalar.copy, h_bf1[:], h32[:, :, halves[1]])
-        interleave(nc.scalar.copy, w_bf[2][:], w_raw[2][:])
-
-        x_sc = sb("x_sc", [P, S], U8, tag="fade3")
-        nc.vector.tensor_copy(x_sc[:], scales_sb[:].indirect(offs_sb[:]))
-        quant_h(0, h_bf0)
-        quant_w(0)
-        quant_w(1)
-        quant_h(1, h_bf1)
-        quant_w(2)
         x_codes = [sb(f"x_codes{g}", [P, S], U32) for g in range(2)]
         for g in range(2):
             for b in range(2):

@@ -27,10 +27,14 @@ def tile_picked_ygrud_cand_p_kernel(
     nc = tc.nc
     with ExitStack() as ctx:
         keep = ctx.enter_context(tc.tile_pool(name="keep", bufs=1))
+        shared = ctx.enter_context(tc.tile_pool(name="shared", bufs=1))
         psum = ctx.enter_context(tc.psum_pool(name="psum", bufs=1))
 
         def sb(name, shape, dtype, tag=None):
             return keep.tile(shape, dtype, name=name, tag=tag or name, align_bytes=64)
+
+        def on_h(name, shape, dtype, offset):
+            return shared.tile(shape, dtype, name=name, tag=name, align_bytes=64, offset=offset)
 
         def interleave(copy, dst, src):
             copy(
@@ -58,9 +62,9 @@ def tile_picked_ygrud_cand_p_kernel(
         def load_w(g):
             nc.sync.dma_start(out=w_raw[g][:], in_=w_src[g].rearrange("(p t) n -> p t n", t=PACK))
 
-        nc.sync.dma_start(slot_sb[:], slot)
-        nc.sync.dma_start(out=mem_sb[0][:], in_=mem_rows[0])
         nc.sync.dma_start(out=gap_col[:], in_=gap[0].rearrange("(p c) -> p c", c=PACK))
+        nc.sync.dma_start(out=mem_sb[0][:], in_=mem_rows[0])
+        nc.sync.dma_start(slot_sb[:], slot)
         nc.sync.dma_start(out=rate_sb[:], in_=rate.rearrange("(p t) o -> p (t o)", t=PACK))
         nc.sync.dma_start(out=off_sb[:], in_=off.rearrange("(p t) o -> p (t o)", t=PACK))
         for t in range(1, PACK):
@@ -96,44 +100,55 @@ def tile_picked_ygrud_cand_p_kernel(
         halves = [slice(b * HALF, (b + 1) * HALF) for b in range(2)]
         offs_half = [offs_sb[:, 16 * b : 16 * (b + 1)] for b in range(2)]
 
-        picked = sb("picked", [P, PACK, S], F32)
-        for t in range(PACK):
+        gap_sb = sb("gap_sb", [P, S], F32)
+        nc.scalar.copy(out=gap_sb[:].rearrange("m (p c) -> m p c", c=PACK), in_=gap_ps[:].rearrange("m c p -> m p c"))
+
+        picked = sb("picked", [P, 2, S], F32)
+        for t in range(2):
             nc.vector.tensor_copy(picked[:, t, :], mem_sb[t][:].indirect(slot_sb[:]))
+        neg_rate = sb("neg_rate", [P, 2], F32)
+        neg_off = sb("neg_off", [P, 2], F32)
+        nc.vector.tensor_scalar_mul(neg_rate[:], rate_sb[:, 0:2], -1.0)
+        nc.vector.tensor_scalar_mul(neg_off[:], off_sb[:, 0:2], -1.0)
+        h_f32 = on_h("h_f32", [P, PACK, S], F32, 0)
 
-        h_codes = sb("h_codes", [P, S], U32)
-        h_sc = sb("h_sc", [P, S], U8)
-        h_bf = []
-        for b in range(2):
-            decay = sb(f"decay{b}", [P, PACK, HALF], F32)
-            fade = sb(f"fade{b}", [P, PACK, HALF], F32)
-            gap_half = gap_ps[:, :, b * P // 2 : (b + 1) * P // 2].rearrange("m c p -> m p c")
-            for t in range(PACK):
-                nc.scalar.activation(
-                    out=decay[:, t, :].rearrange("m (p c) -> m p c", c=PACK), in_=gap_half,
-                    func=ACT.Relu, scale=rate_sb[:, t : t + 1], bias=off_sb[:, t : t + 1],
-                )
-            nc.scalar.activation(out=fade[:], in_=decay[:], func=ACT.Exp, scale=-1.0)
-            h_bf.append(sb(f"h_bf{b}", [P, HALF * PACK], BF16))
-            nc.vector.tensor_tensor(
-                h_bf[b][:].rearrange("p (c i t) -> p c t i", i=4, t=PACK),
-                picked[:, :, halves[b]].rearrange("p t (c i) -> p c t i", i=4),
-                fade[:].rearrange("p t (c i) -> p c t i", i=4),
-                ALU.mult,
+        for t in (2, 3):
+            decay = sb(f"decay{t}", [P, S], F32)
+            fade = sb(f"fade{t}", [P, S], F32)
+            nc.scalar.activation(
+                out=decay[:], in_=gap_sb[:], func=ACT.Relu, scale=rate_sb[:, t : t + 1], bias=off_sb[:, t : t + 1]
             )
-        for b in range(2):
-            nc.vector.quantize_mx(out=h_codes[:, halves[b]].bitcast(FP8X4), scales=h_sc[:, halves[b]], in_=h_bf[b][:])
+            nc.scalar.activation(out=fade[:], in_=decay[:], func=ACT.Exp, scale=-1.0)
+            nc.vector.tensor_tensor(h_f32[:, t, :], mem_sb[t][:].indirect(slot_sb[:]), fade[:], ALU.mult)
+        growth = sb("growth", [P, 2, S], F32)
+        for t in range(2):
+            nc.scalar.activation(
+                out=growth[:, t, :], in_=gap_sb[:], func=ACT.Exp, scale=neg_rate[:, t : t + 1], bias=neg_off[:, t : t + 1]
+            )
+        nc.vector.scalar_tensor_tensor(
+            out=h_f32[:, 0:2, :], in0=growth[:], scalar=1.0, in1=picked[:], op0=ALU.min, op1=ALU.mult
+        )
 
-        x_sc = sb("x_sc", [P, S], U8)
         w_codes = [sb(f"w_codes{g}", [P, N], U32) for g in range(3)]
         w_sc = [sb(f"w_sc{g}", [P, N], U8) for g in range(3)]
-        for g in range(3):
-            w_bf = sb(f"w_bf{g}", [P, N * PACK], BF16)
-            interleave(nc.scalar.copy, w_bf[:], w_raw[g][:])
-            nc.vector.quantize_mx(out=w_codes[g][:].bitcast(FP8X4), scales=w_sc[g][:], in_=w_bf[:])
-            if g == 0:
-                nc.vector.tensor_copy(x_sc[:], scales_sb[:].indirect(offs_sb[:]))
 
-        x_codes = [sb(f"x_codes{g}", [P, S], U32) for g in range(2)]
+        def quantise_w(g, copy, w_bf):
+            interleave(copy, w_bf[:], w_raw[g][:])
+            nc.vector.quantize_mx(out=w_codes[g][:].bitcast(FP8X4), scales=w_sc[g][:], in_=w_bf[:])
+
+        quantise_w(0, nc.scalar.copy, sb("w_bf0", [P, N * PACK], BF16, tag="gap_sb"))
+        x_sc = sb("x_sc", [P, S], U8, tag="picked")
+        nc.vector.tensor_copy(x_sc[:], scales_sb[:].indirect(offs_sb[:]))
+        quantise_w(1, nc.vector.tensor_copy, sb("w_bf1", [P, N * PACK], BF16, tag="growth"))
+        h_codes = sb("h_codes", [P, S], U32)
+        h_sc = sb("h_sc", [P, S], U8)
+        h_bf = sb("h_bf", [P, 2, HALF * PACK], BF16, tag="w_raw0")
+        for b in range(2):
+            interleave(nc.scalar.copy, h_bf[:, b, :], h_f32[:, :, halves[b]])
+            nc.vector.quantize_mx(out=h_codes[:, halves[b]].bitcast(FP8X4), scales=h_sc[:, halves[b]], in_=h_bf[:, b, :])
+        quantise_w(2, nc.scalar.copy, on_h("w_bf2", [P, N * PACK], BF16, 0))
+
+        x_codes = [on_h("x_codes0", [P, S], U32, 2048), sb("x_codes1", [P, S], U32, tag="w_raw2")]
         for g in range(2):
             for b in range(2):
                 nc.vector.tensor_copy(x_codes[g][:, halves[b]], words_sb[g][:].indirect(offs_half[b]))

@@ -27,14 +27,10 @@ def tile_picked_ygrud_cand_p_kernel(
     nc = tc.nc
     with ExitStack() as ctx:
         keep = ctx.enter_context(tc.tile_pool(name="keep", bufs=1))
-        shared = ctx.enter_context(tc.tile_pool(name="shared", bufs=1))
         psum = ctx.enter_context(tc.psum_pool(name="psum", bufs=1))
 
         def sb(name, shape, dtype, tag=None):
             return keep.tile(shape, dtype, name=name, tag=tag or name, align_bytes=64)
-
-        def on_h(name, shape, dtype, offset):
-            return shared.tile(shape, dtype, name=name, tag=name, align_bytes=64, offset=offset)
 
         def interleave(copy, dst, src):
             copy(
@@ -54,6 +50,8 @@ def tile_picked_ygrud_cand_p_kernel(
         w_src = [rr, w1[0:512, :], w1[512:1024, :]]
 
         nc.vector.memset(scales_sb[:].bitcast(I32), 0)
+        x_sc = sb("x_sc", [P, 2, S], U8)
+        nc.vector.memset(x_sc[:].rearrange("p g s -> p (g s)").bitcast(I32), 0)
         ident = sb("ident", [P, P], F32)
         make_identity(nc, ident[:])
 
@@ -67,26 +65,15 @@ def tile_picked_ygrud_cand_p_kernel(
         nc.sync.dma_start(slot_sb[:], slot)
         nc.sync.dma_start(out=rate_sb[:], in_=rate.rearrange("(p t) o -> p (t o)", t=PACK))
         nc.sync.dma_start(out=off_sb[:], in_=off.rearrange("(p t) o -> p (t o)", t=PACK))
-        for t in range(1, PACK):
-            nc.sync.dma_start(out=mem_sb[t][:], in_=mem_rows[t])
+        nc.sync.dma_start(out=mem_sb[1][:], in_=mem_rows[1])
         nc.sync.dma_start(offs_sb[:], offs)
-
-        def load_scales(g, q):
-            nc.sync.dma_start(
-                out=scales_sb[32 * q + 4 * g : 32 * q + 4 * g + 4, :].bitcast(I32),
-                in_=x_scales[g, 4 * q : 4 * q + 4, :].bitcast(I32),
-            )
-
+        nc.sync.dma_start(
+            out=scales_sb[0:P:4, :].bitcast(I32), in_=x_scales.rearrange("g r c -> (g r) c").bitcast(I32)
+        )
+        for t in range(2, PACK):
+            nc.sync.dma_start(out=mem_sb[t][:], in_=mem_rows[t])
         for g in range(3):
             load_w(g)
-            if g < 2:
-                for q in (2, 3):
-                    load_scales(g, q)
-        for q in range(2):
-            nc.gpsimd.dma_start(
-                out=scales_sb[32 * q : 32 * q + 8, :].bitcast(I32),
-                in_=x_scales[:, 4 * q : 4 * q + 4, :].bitcast(I32),
-            )
         for g in range(2):
             nc.sync.dma_start(
                 out=words_sb[g][:].bitcast(I32),
@@ -106,11 +93,19 @@ def tile_picked_ygrud_cand_p_kernel(
         picked = sb("picked", [P, 2, S], F32)
         for t in range(2):
             nc.vector.tensor_copy(picked[:, t, :], mem_sb[t][:].indirect(slot_sb[:]))
+        sc_rows = sb("sc_rows", [P, S], U8)
+        nc.vector.tensor_copy(sc_rows[:], scales_sb[:].indirect(offs_sb[:]))
+        for g, queue in enumerate((nc.gpsimd, nc.sync)):
+            for q in range(4):
+                first = 4 * (16 * g + 4 * q)
+                queue.dma_start(
+                    out=x_sc[32 * q : 32 * q + 4, g, :].bitcast(I32), in_=sc_rows[first : first + 16 : 4, :].bitcast(I32)
+                )
         neg_rate = sb("neg_rate", [P, 2], F32)
         neg_off = sb("neg_off", [P, 2], F32)
         nc.vector.tensor_scalar_mul(neg_rate[:], rate_sb[:, 0:2], -1.0)
         nc.vector.tensor_scalar_mul(neg_off[:], off_sb[:, 0:2], -1.0)
-        h_f32 = on_h("h_f32", [P, PACK, S], F32, 0)
+        h_f32 = sb("h_f32", [P, PACK, S], F32)
 
         for t in (2, 3):
             decay = sb(f"decay{t}", [P, S], F32)
@@ -129,43 +124,41 @@ def tile_picked_ygrud_cand_p_kernel(
             out=h_f32[:, 0:2, :], in0=growth[:], scalar=1.0, in1=picked[:], op0=ALU.min, op1=ALU.mult
         )
 
-        w_codes = [sb(f"w_codes{g}", [P, N], U32) for g in range(3)]
+        w_codes = [sb(f"w_codes{g}", [P, N], U32, tag=("fade3", "w_codes1", "w_codes2")[g]) for g in range(3)]
         w_sc = [sb(f"w_sc{g}", [P, N], U8) for g in range(3)]
 
         def quantise_w(g, copy, w_bf):
-            interleave(copy, w_bf[:], w_raw[g][:])
-            nc.vector.quantize_mx(out=w_codes[g][:].bitcast(FP8X4), scales=w_sc[g][:], in_=w_bf[:])
+            interleave(copy, w_bf, w_raw[g][:])
+            nc.vector.quantize_mx(out=w_codes[g][:].bitcast(FP8X4), scales=w_sc[g][:], in_=w_bf)
 
-        quantise_w(0, nc.scalar.copy, sb("w_bf0", [P, N * PACK], BF16, tag="gap_sb"))
-        x_sc = sb("x_sc", [P, S], U8, tag="picked")
-        nc.vector.tensor_copy(x_sc[:], scales_sb[:].indirect(offs_sb[:]))
-        quantise_w(1, nc.vector.tensor_copy, sb("w_bf1", [P, N * PACK], BF16, tag="growth"))
+        w_bf = sb("w_bf", [P, 3, N * PACK], BF16, tag="gap_sb")
+        for g in range(3):
+            quantise_w(g, nc.scalar.copy, w_bf[:, g, :])
+        x_codes = [sb(f"x_codes{g}", [P, S], U32, tag=("gap_sb", "h_f32")[g]) for g in range(2)]
+        for b in range(2):
+            nc.vector.tensor_copy(x_codes[0][:, halves[b]], words_sb[0][:].indirect(offs_half[b]))
         h_codes = sb("h_codes", [P, S], U32)
         h_sc = sb("h_sc", [P, S], U8)
-        h_bf = sb("h_bf", [P, 2, HALF * PACK], BF16, tag="w_raw0")
+        h_bf = sb("h_bf", [P, 2, HALF * PACK], BF16, tag="w_raw2")
         for b in range(2):
             interleave(nc.scalar.copy, h_bf[:, b, :], h_f32[:, :, halves[b]])
             nc.vector.quantize_mx(out=h_codes[:, halves[b]].bitcast(FP8X4), scales=h_sc[:, halves[b]], in_=h_bf[:, b, :])
-        quantise_w(2, nc.scalar.copy, on_h("w_bf2", [P, N * PACK], BF16, 0))
-
-        x_codes = [on_h("x_codes0", [P, S], U32, 2048), sb("x_codes1", [P, S], U32, tag="w_raw2")]
-        for g in range(2):
-            for b in range(2):
-                nc.vector.tensor_copy(x_codes[g][:, halves[b]], words_sb[g][:].indirect(offs_half[b]))
+        for b in range(2):
+            nc.vector.tensor_copy(x_codes[1][:, halves[b]], words_sb[1][:].indirect(offs_half[b]))
         x0, x1 = x_codes
 
         acc = [[psum.tile([P, HALF], F32, name=f"acc{b}{m}") for m in range(2)] for b in range(2)]
-        moving = [(h_codes, h_sc, 0), (x0, x_sc, 0), (x1, x_sc, 4)]
-        for g, (codes, scales, row0) in enumerate(moving):
+        moving = [(1, x0[:], x_sc[:, 0, :]), (0, h_codes[:], h_sc[:]), (2, x1[:], x_sc[:, 1, :])]
+        for step, (g, codes, scales) in enumerate(moving):
             for b in range(2):
                 for m in range(2):
                     cols = slice(m * P, (m + 1) * P)
                     nc.tensor.matmul_mx(
                         out=acc[b][m][:], lhsT=w_codes[g][:, cols].bitcast(FP8X4), lhsT_scale=w_sc[g][:, cols],
-                        rhs=codes[:, halves[b]].bitcast(FP8X4), rhs_scale=scales[row0:P, halves[b]],
-                        start=(g == 0), stop=(g == 2),
+                        rhs=codes[:, halves[b]].bitcast(FP8X4), rhs_scale=scales[:, halves[b]],
+                        start=(step == 0), stop=(step == 2),
                     )
-                    if g == 2:
+                    if step == 2:
                         res = sb(f"res{b}{m}", [P, HALF], F32)
                         nc.scalar.activation(out=res[:], in_=acc[b][m][:], func=ACT.Tanh)
                         nc.sync.dma_start(out=out[cols, halves[b]], in_=res[:])

@@ -68,7 +68,7 @@ def tile_picked_ygrud_cand_p_kernel(
         nc.sync.dma_start(out=mem_sb[1][:], in_=mem_rows[1])
         nc.sync.dma_start(offs_sb[:], offs)
         nc.sync.dma_start(
-            out=scales_sb[0:P:4, :].bitcast(I32), in_=x_scales.rearrange("g r c -> (g r) c").bitcast(I32)
+            out=scales_sb[0:P:4, :].bitcast(I32), in_=x_scales.rearrange("g r c -> r g c").bitcast(I32)
         )
         for t in range(2, PACK):
             nc.sync.dma_start(out=mem_sb[t][:], in_=mem_rows[t])
@@ -95,12 +95,11 @@ def tile_picked_ygrud_cand_p_kernel(
             nc.vector.tensor_copy(picked[:, t, :], mem_sb[t][:].indirect(slot_sb[:]))
         sc_rows = sb("sc_rows", [P, S], U8)
         nc.vector.tensor_copy(sc_rows[:], scales_sb[:].indirect(offs_sb[:]))
-        for g, queue in enumerate((nc.gpsimd, nc.sync)):
-            for q in range(4):
-                first = 4 * (16 * g + 4 * q)
-                queue.dma_start(
-                    out=x_sc[32 * q : 32 * q + 4, g, :].bitcast(I32), in_=sc_rows[first : first + 16 : 4, :].bitcast(I32)
-                )
+        for q in range(4):
+            nc.gpsimd.dma_start(
+                out=x_sc[32 * q : 32 * q + 4, :, :].rearrange("p g s -> p (g s)").bitcast(I32),
+                in_=sc_rows[32 * q : 32 * q + 32 : 4, :].bitcast(I32),
+            )
         neg_rate = sb("neg_rate", [P, 2], F32)
         neg_off = sb("neg_off", [P, 2], F32)
         nc.vector.tensor_scalar_mul(neg_rate[:], rate_sb[:, 0:2], -1.0)

@@ -27,6 +27,7 @@ def tile_picked_ygrud_cand_p_kernel(
     nc = tc.nc
     with ExitStack() as ctx:
         keep = ctx.enter_context(tc.tile_pool(name="keep", bufs=1))
+        shared = ctx.enter_context(tc.tile_pool(name="shared", bufs=1))
         psum = ctx.enter_context(tc.psum_pool(name="psum", bufs=1))
 
         def sb(name, shape, dtype, tag=None):
@@ -44,9 +45,12 @@ def tile_picked_ygrud_cand_p_kernel(
         rate_sb = sb("rate_sb", [P, PACK], F32)
         off_sb = sb("off_sb", [P, PACK], F32)
         mem_sb = [sb(f"mem{t}", [P, U], F32) for t in range(PACK)]
-        words_sb = [sb(f"words{g}", [P, T], U32) for g in range(2)]
-        scales_sb = sb("scales_sb", [P, T], U8)
-        w_raw = [sb(f"w_raw{g}", [P, PACK, N], F32) for g in range(3)]
+        scales_sb = shared.tile([P, T], U8, name="scales_sb", align_bytes=64, offset=4 * T - T // 2)
+
+        def on_w1(name, shape, dtype, offset):
+            return shared.tile(shape, dtype, name=name, align_bytes=64, offset=8 * T + offset)
+
+        w_raw = [sb("w_raw0", [P, PACK, N], F32), on_w1("w_raw1", [P, PACK, N], F32, 0), sb("w_raw2", [P, PACK, N], F32)]
         w_src = [rr, w1[0:512, :], w1[512:1024, :]]
 
         nc.vector.memset(scales_sb[:].bitcast(I32), 0)
@@ -74,11 +78,6 @@ def tile_picked_ygrud_cand_p_kernel(
             nc.sync.dma_start(out=mem_sb[t][:], in_=mem_rows[t])
         for g in range(3):
             load_w(g)
-        for g in range(2):
-            nc.sync.dma_start(
-                out=words_sb[g][:].bitcast(I32),
-                in_=x_words[g].rearrange("p n t -> p (n t)").bitcast(I32),
-            )
 
         gap_ps = psum.tile([P, PACK, P], F32, name="gap_ps")
         for c in range(PACK):
@@ -96,10 +95,19 @@ def tile_picked_ygrud_cand_p_kernel(
         sc_rows = sb("sc_rows", [P, S], U8)
         nc.vector.tensor_copy(sc_rows[:], scales_sb[:].indirect(offs_sb[:]))
         for q in range(4):
-            nc.gpsimd.dma_start(
+            nc.sync.dma_start(
                 out=x_sc[32 * q : 32 * q + 4, :, :].rearrange("p g s -> p (g s)").bitcast(I32),
                 in_=sc_rows[32 * q : 32 * q + 32 : 4, :].bitcast(I32),
             )
+        words_sb = [
+            shared.tile([P, T], U32, name=f"words{g}", align_bytes=64, offset=4 * T * g) for g in range(2)
+        ]
+        for g in range(2):
+            nc.sync.dma_start(
+                out=words_sb[g][:].bitcast(I32),
+                in_=x_words[g].rearrange("p n t -> p (n t)").bitcast(I32),
+            )
+
         neg_rate = sb("neg_rate", [P, 2], F32)
         neg_off = sb("neg_off", [P, 2], F32)
         nc.vector.tensor_scalar_mul(neg_rate[:], rate_sb[:, 0:2], -1.0)
@@ -130,24 +138,24 @@ def tile_picked_ygrud_cand_p_kernel(
             interleave(copy, w_bf, w_raw[g][:])
             nc.vector.quantize_mx(out=w_codes[g][:].bitcast(FP8X4), scales=w_sc[g][:], in_=w_bf)
 
-        w_bf = sb("w_bf", [P, 3, N * PACK], BF16, tag="gap_sb")
-        for g in range(3):
+        w_bf = sb("w_bf", [P, 2, N * PACK], BF16, tag="gap_sb")
+        for g in range(2):
             quantise_w(g, nc.scalar.copy, w_bf[:, g, :])
-        x_codes = [sb(f"x_codes{g}", [P, S], U32, tag=("gap_sb", "h_f32")[g]) for g in range(2)]
-        for b in range(2):
-            nc.vector.tensor_copy(x_codes[0][:, halves[b]], words_sb[0][:].indirect(offs_half[b]))
+        quantise_w(2, nc.vector.tensor_copy, sb("w_bf2", [P, N * PACK], BF16, tag="growth")[:])
         h_codes = sb("h_codes", [P, S], U32)
         h_sc = sb("h_sc", [P, S], U8)
-        h_bf = sb("h_bf", [P, 2, HALF * PACK], BF16, tag="w_raw2")
         for b in range(2):
-            interleave(nc.scalar.copy, h_bf[:, b, :], h_f32[:, :, halves[b]])
-            nc.vector.quantize_mx(out=h_codes[:, halves[b]].bitcast(FP8X4), scales=h_sc[:, halves[b]], in_=h_bf[:, b, :])
-        for b in range(2):
-            nc.vector.tensor_copy(x_codes[1][:, halves[b]], words_sb[1][:].indirect(offs_half[b]))
+            h_bf = on_w1(f"h_bf{b}", [P, HALF * PACK], BF16, 2048 * b)
+            interleave(nc.scalar.copy, h_bf[:], h_f32[:, :, halves[b]])
+            nc.vector.quantize_mx(out=h_codes[:, halves[b]].bitcast(FP8X4), scales=h_sc[:, halves[b]], in_=h_bf[:])
+        x_codes = [on_w1("x_codes0", [P, S], U32, 0), sb("x_codes1", [P, S], U32, tag="h_f32")]
+        for g in range(2):
+            for b in range(2):
+                nc.vector.tensor_copy(x_codes[g][:, halves[b]], words_sb[g][:].indirect(offs_half[b]))
         x0, x1 = x_codes
 
         acc = [[psum.tile([P, HALF], F32, name=f"acc{b}{m}") for m in range(2)] for b in range(2)]
-        moving = [(1, x0[:], x_sc[:, 0, :]), (0, h_codes[:], h_sc[:]), (2, x1[:], x_sc[:, 1, :])]
+        moving = [(0, h_codes[:], h_sc[:]), (1, x0[:], x_sc[:, 0, :]), (2, x1[:], x_sc[:, 1, :])]
         for step, (g, codes, scales) in enumerate(moving):
             for b in range(2):
                 for m in range(2):

@@ -42,8 +42,7 @@ def tile_picked_ygrud_cand_p_kernel(
         offs_sb = sb("offs_sb", [P, S // 16], U16)
         slot_sb = sb("slot_sb", [P, S // 16], U16)
         gap_col = sb("gap_col", [P, PACK], F32)
-        rate_sb = sb("rate_sb", [P, PACK], F32)
-        off_sb = sb("off_sb", [P, PACK], F32)
+        rows_sb = sb("rows_sb", [P, H], F32)
         mem_sb = [sb(f"mem{t}", [P, U], F32) for t in range(PACK)]
         scales_sb = shared.tile([P, T], U8, name="scales_sb", align_bytes=64, offset=4 * T - T // 2)
 
@@ -53,6 +52,7 @@ def tile_picked_ygrud_cand_p_kernel(
         w_raw = [sb("w_raw0", [P, PACK, N], F32), on_w1("w_raw1", [P, PACK, N], F32, 0), sb("w_raw2", [P, PACK, N], F32)]
         w_src = [rr, w1[0:512, :], w1[512:1024, :]]
 
+        nc.vector.memset(rows_sb[:], 0.0)
         nc.vector.memset(scales_sb[:].bitcast(I32), 0)
         x_sc = sb("x_sc", [P, 2, S], U8)
         nc.vector.memset(x_sc[:].rearrange("p g s -> p (g s)").bitcast(I32), 0)
@@ -67,8 +67,8 @@ def tile_picked_ygrud_cand_p_kernel(
         nc.sync.dma_start(out=gap_col[:], in_=gap[0].rearrange("(p c) -> p c", c=PACK))
         nc.sync.dma_start(out=mem_sb[0][:], in_=mem_rows[0])
         nc.sync.dma_start(slot_sb[:], slot)
-        nc.sync.dma_start(out=rate_sb[:], in_=rate.rearrange("(p t) o -> p (t o)", t=PACK))
-        nc.sync.dma_start(out=off_sb[:], in_=off.rearrange("(p t) o -> p (t o)", t=PACK))
+        nc.sync.dma_start(out=rows_sb[0:1, :], in_=rate.rearrange("k o -> o k"))
+        nc.sync.dma_start(out=rows_sb[1:2, :], in_=off.rearrange("k o -> o k"))
         nc.sync.dma_start(out=mem_sb[1][:], in_=mem_rows[1])
         nc.sync.dma_start(offs_sb[:], offs)
         nc.sync.dma_start(
@@ -86,8 +86,16 @@ def tile_picked_ygrud_cand_p_kernel(
         halves = [slice(b * HALF, (b + 1) * HALF) for b in range(2)]
         offs_half = [offs_sb[:, 16 * b : 16 * (b + 1)] for b in range(2)]
 
-        gap_sb = sb("gap_sb", [P, S], F32)
-        nc.scalar.copy(out=gap_sb[:].rearrange("m (p c) -> m p c", c=PACK), in_=gap_ps[:].rearrange("m c p -> m p c"))
+        coef_ps = {first: psum.tile([P, 2, P], F32, name=f"coef_ps{first}") for first in (2, 0)}
+        for first in (2, 0):
+            for t in range(2):
+                nc.tensor.transpose(coef_ps[first][:, t, :], rows_sb[:, first + t : H : PACK], ident[:])
+        coef = sb("coef", [P, 2, 2], F32)
+        nc.scalar.copy(out=coef[:], in_=coef_ps[2][:, :, 0:2])
+        gap_all = gap_ps[:].rearrange("m c p -> m p c")
+
+        def by_column(ap):
+            return ap.rearrange("m (p c) -> m p c", c=PACK)
 
         picked = sb("picked", [P, 2, S], F32)
         for t in range(2):
@@ -108,24 +116,23 @@ def tile_picked_ygrud_cand_p_kernel(
                 in_=x_words[g].rearrange("p n t -> p (n t)").bitcast(I32),
             )
 
-        neg_rate = sb("neg_rate", [P, 2], F32)
-        neg_off = sb("neg_off", [P, 2], F32)
-        nc.vector.tensor_scalar_mul(neg_rate[:], rate_sb[:, 0:2], -1.0)
-        nc.vector.tensor_scalar_mul(neg_off[:], off_sb[:, 0:2], -1.0)
+        neg_coef = sb("neg_coef", [P, 2, 2], F32, tag="mem1")
+        nc.vector.tensor_scalar_mul(neg_coef[:], coef_ps[0][:, :, 0:2], -1.0)
         h_f32 = sb("h_f32", [P, PACK, S], F32)
 
         for t in (2, 3):
             decay = sb(f"decay{t}", [P, S], F32)
             fade = sb(f"fade{t}", [P, S], F32)
             nc.scalar.activation(
-                out=decay[:], in_=gap_sb[:], func=ACT.Relu, scale=rate_sb[:, t : t + 1], bias=off_sb[:, t : t + 1]
+                out=by_column(decay[:]), in_=gap_all, func=ACT.Relu, scale=coef[:, t - 2, 0:1], bias=coef[:, t - 2, 1:2]
             )
             nc.scalar.activation(out=fade[:], in_=decay[:], func=ACT.Exp, scale=-1.0)
             nc.vector.tensor_tensor(h_f32[:, t, :], mem_sb[t][:].indirect(slot_sb[:]), fade[:], ALU.mult)
         growth = sb("growth", [P, 2, S], F32)
         for t in range(2):
             nc.scalar.activation(
-                out=growth[:, t, :], in_=gap_sb[:], func=ACT.Exp, scale=neg_rate[:, t : t + 1], bias=neg_off[:, t : t + 1]
+                out=by_column(growth[:, t, :]), in_=gap_all, func=ACT.Exp,
+                scale=neg_coef[:, t, 0:1], bias=neg_coef[:, t, 1:2],
             )
         nc.vector.scalar_tensor_tensor(
             out=h_f32[:, 0:2, :], in0=growth[:], scalar=1.0, in1=picked[:], op0=ALU.min, op1=ALU.mult
@@ -138,7 +145,7 @@ def tile_picked_ygrud_cand_p_kernel(
             interleave(copy, w_bf, w_raw[g][:])
             nc.vector.quantize_mx(out=w_codes[g][:].bitcast(FP8X4), scales=w_sc[g][:], in_=w_bf)
 
-        w_bf = sb("w_bf", [P, 2, N * PACK], BF16, tag="gap_sb")
+        w_bf = sb("w_bf", [P, 2, N * PACK], BF16, tag="mem1")
         for g in range(2):
             quantise_w(g, nc.scalar.copy, w_bf[:, g, :])
         quantise_w(2, nc.vector.tensor_copy, sb("w_bf2", [P, N * PACK], BF16, tag="growth")[:])

@@ -27,7 +27,6 @@ def tile_picked_ygrud_cand_p_kernel(
     nc = tc.nc
     with ExitStack() as ctx:
         keep = ctx.enter_context(tc.tile_pool(name="keep", bufs=1))
-        shared = ctx.enter_context(tc.tile_pool(name="shared", bufs=1))
         psum = ctx.enter_context(tc.psum_pool(name="psum", bufs=1))
 
         def sb(name, shape, dtype, tag=None):
@@ -44,12 +43,8 @@ def tile_picked_ygrud_cand_p_kernel(
         gap_col = sb("gap_col", [P, PACK], F32)
         rows_sb = sb("rows_sb", [P, H], F32)
         mem_sb = [sb(f"mem{t}", [P, U], F32) for t in range(PACK)]
-        scales_sb = shared.tile([P, T], U8, name="scales_sb", align_bytes=64, offset=4 * T - T // 2)
-
-        def on_w1(name, shape, dtype, offset):
-            return shared.tile(shape, dtype, name=name, align_bytes=64, offset=8 * T + offset)
-
-        w_raw = [sb("w_raw0", [P, PACK, N], F32), on_w1("w_raw1", [P, PACK, N], F32, 0), sb("w_raw2", [P, PACK, N], F32)]
+        scales_sb = sb("scales_sb", [P, T], U8)
+        w_raw = [sb(f"w_raw{g}", [P, PACK, N], F32) for g in range(3)]
         w_src = [rr, w1[0:512, :], w1[512:1024, :]]
 
         nc.vector.memset(rows_sb[:], 0.0)
@@ -79,6 +74,13 @@ def tile_picked_ygrud_cand_p_kernel(
         for g in range(3):
             load_w(g)
 
+        def load_words(g, reuse):
+            words = sb(f"words{g}", [P, T], U32, tag=reuse)
+            nc.sync.dma_start(out=words[:].bitcast(I32), in_=x_words[g].rearrange("p n t -> p (n t)").bitcast(I32))
+            return words
+
+        words_sb = [load_words(0, None)]
+
         gap_ps = psum.tile([P, PACK, P], F32, name="gap_ps")
         for c in range(PACK):
             nc.tensor.transpose(gap_ps[:, c, :], gap_col[:, c : c + 1].to_broadcast([P, P]), ident[:])
@@ -107,15 +109,7 @@ def tile_picked_ygrud_cand_p_kernel(
                 out=x_sc[32 * q : 32 * q + 4, :, :].rearrange("p g s -> p (g s)").bitcast(I32),
                 in_=sc_rows[32 * q : 32 * q + 32 : 4, :].bitcast(I32),
             )
-        words_sb = [
-            shared.tile([P, T], U32, name=f"words{g}", align_bytes=64, offset=4 * T * g) for g in range(2)
-        ]
-        for g in range(2):
-            nc.sync.dma_start(
-                out=words_sb[g][:].bitcast(I32),
-                in_=x_words[g].rearrange("p n t -> p (n t)").bitcast(I32),
-            )
-
+        words_sb.append(load_words(1, "scales_sb"))
         neg_coef = sb("neg_coef", [P, 2, 2], F32, tag="mem1")
         nc.vector.tensor_scalar_mul(neg_coef[:], coef_ps[0][:, :, 0:2], -1.0)
         h_f32 = sb("h_f32", [P, PACK, S], F32)
@@ -145,21 +139,26 @@ def tile_picked_ygrud_cand_p_kernel(
             interleave(copy, w_bf, w_raw[g][:])
             nc.vector.quantize_mx(out=w_codes[g][:].bitcast(FP8X4), scales=w_sc[g][:], in_=w_bf)
 
-        w_bf = sb("w_bf", [P, 2, N * PACK], BF16, tag="mem1")
+        w_bf = sb("w_bf", [P, 2, N * PACK], BF16, tag="fade2")
         for g in range(2):
             quantise_w(g, nc.scalar.copy, w_bf[:, g, :])
-        quantise_w(2, nc.vector.tensor_copy, sb("w_bf2", [P, N * PACK], BF16, tag="growth")[:])
         h_codes = sb("h_codes", [P, S], U32)
         h_sc = sb("h_sc", [P, S], U8)
+        h_bf = [sb(f"h_bf{b}", [P, HALF * PACK], BF16, tag=("w_raw0", "h_bf1")[b]) for b in range(2)]
+        for b, copy in enumerate((nc.scalar.copy, nc.vector.tensor_copy)):
+            interleave(copy, h_bf[b][:], h_f32[:, :, halves[b]])
         for b in range(2):
-            h_bf = on_w1(f"h_bf{b}", [P, HALF * PACK], BF16, 2048 * b)
-            interleave(nc.scalar.copy, h_bf[:], h_f32[:, :, halves[b]])
-            nc.vector.quantize_mx(out=h_codes[:, halves[b]].bitcast(FP8X4), scales=h_sc[:, halves[b]], in_=h_bf[:])
-        x_codes = [on_w1("x_codes0", [P, S], U32, 0), sb("x_codes1", [P, S], U32, tag="h_f32")]
-        for g in range(2):
+            nc.vector.quantize_mx(out=h_codes[:, halves[b]].bitcast(FP8X4), scales=h_sc[:, halves[b]], in_=h_bf[b][:])
+
+        def gather_words(g, codes):
             for b in range(2):
-                nc.vector.tensor_copy(x_codes[g][:, halves[b]], words_sb[g][:].indirect(offs_half[b]))
-        x0, x1 = x_codes
+                nc.vector.tensor_copy(codes[:, halves[b]], words_sb[g][:].indirect(offs_half[b]))
+
+        x0 = sb("x_codes0", [P, S], U32, tag="h_f32")
+        gather_words(0, x0)
+        quantise_w(2, nc.scalar.copy, sb("w_bf2", [P, N * PACK], BF16, tag="growth")[:])
+        x1 = sb("x_codes1", [P, S], U32, tag="w_raw2")
+        gather_words(1, x1)
 
         acc = [[psum.tile([P, HALF], F32, name=f"acc{b}{m}") for m in range(2)] for b in range(2)]
         moving = [(0, h_codes[:], h_sc[:]), (1, x0[:], x_sc[:, 0, :]), (2, x1[:], x_sc[:, 1, :])]

@@ -81,7 +81,7 @@ def tile_picked_ygrud_cand_p_kernel(
 
         words_sb = [load_words(0, None)]
 
-        gap_ps = psum.tile([P, PACK, P], F32, name="gap_ps")
+        gap_ps = psum.tile([P, PACK, P], F32, name="gap_ps", tag="gap_ps")
         for c in range(PACK):
             nc.tensor.transpose(gap_ps[:, c, :], gap_col[:, c : c + 1].to_broadcast([P, P]), ident[:])
 
@@ -104,12 +104,17 @@ def tile_picked_ygrud_cand_p_kernel(
             nc.vector.tensor_copy(picked[:, t, :], mem_sb[t][:].indirect(slot_sb[:]))
         sc_rows = sb("sc_rows", [P, S], U8)
         nc.vector.tensor_copy(sc_rows[:], scales_sb[:].indirect(offs_sb[:]))
-        for q in range(4):
-            nc.sync.dma_start(
-                out=x_sc[32 * q : 32 * q + 4, :, :].rearrange("p g s -> p (g s)").bitcast(I32),
-                in_=sc_rows[32 * q : 32 * q + 32 : 4, :].bitcast(I32),
-            )
+
+        def move_scales(g):
+            for q in range(4):
+                nc.sync.dma_start(
+                    out=x_sc[32 * q : 32 * q + 4, g, :].bitcast(I32),
+                    in_=sc_rows[32 * q + 4 * g : 32 * q + 32 : 8, :].bitcast(I32),
+                )
+
+        move_scales(0)
         words_sb.append(load_words(1, "scales_sb"))
+        move_scales(1)
         neg_coef = sb("neg_coef", [P, 2, 2], F32, tag="mem1")
         nc.vector.tensor_scalar_mul(neg_coef[:], coef_ps[0][:, :, 0:2], -1.0)
         h_f32 = sb("h_f32", [P, PACK, S], F32)
@@ -160,18 +165,22 @@ def tile_picked_ygrud_cand_p_kernel(
         x1 = sb("x_codes1", [P, S], U32, tag="w_raw2")
         gather_words(1, x1)
 
-        acc = [[psum.tile([P, HALF], F32, name=f"acc{b}{m}") for m in range(2)] for b in range(2)]
+        pieces = [(0, slice(0, P)), (0, slice(P, HALF)), (1, halves[0]), (0, halves[1]), (1, halves[1])]
+        banks = ["acc0", "gap_ps", "acc1", "acc2", "acc3"]
+        acc = [
+            psum.tile([P, cols.stop - cols.start], F32, name=f"acc_piece{i}", tag=banks[i])
+            for i, (m, cols) in enumerate(pieces)
+        ]
         moving = [(0, h_codes[:], h_sc[:]), (1, x0[:], x_sc[:, 0, :]), (2, x1[:], x_sc[:, 1, :])]
         for step, (g, codes, scales) in enumerate(moving):
-            for b in range(2):
-                for m in range(2):
-                    cols = slice(m * P, (m + 1) * P)
-                    nc.tensor.matmul_mx(
-                        out=acc[b][m][:], lhsT=w_codes[g][:, cols].bitcast(FP8X4), lhsT_scale=w_sc[g][:, cols],
-                        rhs=codes[:, halves[b]].bitcast(FP8X4), rhs_scale=scales[:, halves[b]],
-                        start=(step == 0), stop=(step == 2),
-                    )
-                    if step == 2:
-                        res = sb(f"res{b}{m}", [P, HALF], F32)
-                        nc.scalar.activation(out=res[:], in_=acc[b][m][:], func=ACT.Tanh)
-                        nc.sync.dma_start(out=out[cols, halves[b]], in_=res[:])
+            for i, (m, cols) in enumerate(pieces):
+                rows = slice(m * P, (m + 1) * P)
+                nc.tensor.matmul_mx(
+                    out=acc[i][:], lhsT=w_codes[g][:, rows].bitcast(FP8X4), lhsT_scale=w_sc[g][:, rows],
+                    rhs=codes[:, cols].bitcast(FP8X4), rhs_scale=scales[:, cols],
+                    start=(step == 0), stop=(step == 2),
+                )
+                if step == 2:
+                    res = sb(f"res{i}", [P, cols.stop - cols.start], F32)
+                    nc.scalar.activation(out=res[:], in_=acc[i][:], func=ACT.Tanh)
+                    nc.sync.dma_start(out=out[rows, cols], in_=res[:])

@@ -104,17 +104,12 @@ def tile_picked_ygrud_cand_p_kernel(
             nc.vector.tensor_copy(picked[:, t, :], mem_sb[t][:].indirect(slot_sb[:]))
         sc_rows = sb("sc_rows", [P, S], U8)
         nc.vector.tensor_copy(sc_rows[:], scales_sb[:].indirect(offs_sb[:]))
-
-        def move_scales(g):
-            for q in range(4):
-                nc.sync.dma_start(
-                    out=x_sc[32 * q : 32 * q + 4, g, :].bitcast(I32),
-                    in_=sc_rows[32 * q + 4 * g : 32 * q + 32 : 8, :].bitcast(I32),
-                )
-
-        move_scales(0)
+        for q in range(4):
+            nc.sync.dma_start(
+                out=x_sc[32 * q : 32 * q + 4, :, :].rearrange("p g s -> p (g s)").bitcast(I32),
+                in_=sc_rows[32 * q : 32 * q + 32 : 4, :].bitcast(I32),
+            )
         words_sb.append(load_words(1, "scales_sb"))
-        move_scales(1)
         neg_coef = sb("neg_coef", [P, 2, 2], F32, tag="mem1")
         nc.vector.tensor_scalar_mul(neg_coef[:], coef_ps[0][:, :, 0:2], -1.0)
         h_f32 = sb("h_f32", [P, PACK, S], F32)

@@ -42,36 +42,35 @@ def tile_picked_ygrud_cand_p_kernel(
         slot_sb = sb("slot_sb", [P, S // 16], U16)
         gap_col = sb("gap_col", [P, PACK], F32)
         rows_sb = sb("rows_sb", [P, H], F32)
-        mem_sb = [sb(f"mem{t}", [P, U], F32) for t in range(PACK)]
+        mem_pair = [sb(f"mem{a}", [P, 2 * U], F32) for a in range(2)]
         scales_sb = sb("scales_sb", [P, T], U8)
         w_raw = [sb(f"w_raw{g}", [P, PACK, N], F32) for g in range(3)]
         w_src = [rr, w1[0:512, :], w1[512:1024, :]]
-
-        nc.vector.memset(rows_sb[:], 0.0)
-        nc.vector.memset(scales_sb[:].bitcast(I32), 0)
         x_sc = sb("x_sc", [P, 2, S], U8)
-        nc.vector.memset(x_sc[:].rearrange("p g s -> p (g s)").bitcast(I32), 0)
         ident = sb("ident", [P, P], F32)
+
+        nc.gpsimd.memset(rows_sb[:], 0.0)
+        nc.vector.memset(scales_sb[:].bitcast(I32), 0)
+        nc.vector.memset(x_sc[:].rearrange("p g s -> p (g s)").bitcast(I32), 0)
         make_identity(nc, ident[:])
 
-        mem_rows = mem.rearrange("(p t) u -> t p u", t=PACK)
+        mem_rows = mem.rearrange("(p a t) u -> a p (t u)", a=2, t=2)
 
         def load_w(g):
             nc.sync.dma_start(out=w_raw[g][:], in_=w_src[g].rearrange("(p t) n -> p t n", t=PACK))
 
+        load_w(0)
         nc.sync.dma_start(out=gap_col[:], in_=gap[0].rearrange("(p c) -> p c", c=PACK))
-        nc.sync.dma_start(out=mem_sb[0][:], in_=mem_rows[0])
+        nc.sync.dma_start(offs_sb[:], offs)
         nc.sync.dma_start(slot_sb[:], slot)
         nc.sync.dma_start(out=rows_sb[0:1, :], in_=rate.rearrange("k o -> o k"))
         nc.sync.dma_start(out=rows_sb[1:2, :], in_=off.rearrange("k o -> o k"))
-        nc.sync.dma_start(out=mem_sb[1][:], in_=mem_rows[1])
-        nc.sync.dma_start(offs_sb[:], offs)
         nc.sync.dma_start(
             out=scales_sb[0:P:4, :].bitcast(I32), in_=x_scales.rearrange("g r c -> r g c").bitcast(I32)
         )
-        for t in range(2, PACK):
-            nc.sync.dma_start(out=mem_sb[t][:], in_=mem_rows[t])
-        for g in range(3):
+        for a in range(2):
+            nc.sync.dma_start(out=mem_pair[a][:], in_=mem_rows[a])
+        for g in (1, 2):
             load_w(g)
 
         def load_words(g, reuse):
@@ -84,69 +83,70 @@ def tile_picked_ygrud_cand_p_kernel(
         gap_ps = psum.tile([P, PACK, P], F32, name="gap_ps", tag="gap_ps")
         for c in range(PACK):
             nc.tensor.transpose(gap_ps[:, c, :], gap_col[:, c : c + 1].to_broadcast([P, P]), ident[:])
-
-        halves = [slice(b * HALF, (b + 1) * HALF) for b in range(2)]
-        offs_half = [offs_sb[:, 16 * b : 16 * (b + 1)] for b in range(2)]
-
-        coef_ps = {first: psum.tile([P, 2, P], F32, name=f"coef_ps{first}") for first in (2, 0)}
-        for first in (2, 0):
-            for t in range(2):
-                nc.tensor.transpose(coef_ps[first][:, t, :], rows_sb[:, first + t : H : PACK], ident[:])
-        coef = sb("coef", [P, 2, 2], F32)
-        nc.scalar.copy(out=coef[:], in_=coef_ps[2][:, :, 0:2])
+        coef_ps = psum.tile([P, PACK, P], F32, name="coef_ps")
+        for t in range(PACK):
+            nc.tensor.transpose(coef_ps[:, t, :], rows_sb[:, t:H:PACK], ident[:])
+        neg_coef = sb("neg_coef", [P, PACK, 2], F32)
+        nc.scalar.activation(out=neg_coef[:], in_=coef_ps[:, :, 0:2], func=ACT.Copy, scale=-1.0)
         gap_all = gap_ps[:].rearrange("m c p -> m p c")
 
         def by_column(ap):
             return ap.rearrange("m (p c) -> m p c", c=PACK)
 
-        picked = sb("picked", [P, 2, S], F32)
-        for t in range(2):
-            nc.vector.tensor_copy(picked[:, t, :], mem_sb[t][:].indirect(slot_sb[:]))
+        halves = [slice(b * HALF, (b + 1) * HALF) for b in range(2)]
+        offs_half = [offs_sb[:, 16 * b : 16 * (b + 1)] for b in range(2)]
+
+        w_codes = []
+        w_sc = [sb(f"w_sc{g}", [P, N], U8) for g in range(3)]
+
+        def quantise_w(g, w_bf, reuse=None):
+            w_codes.append(sb(f"w_codes{g}", [P, N], U32, tag=reuse))
+            nc.vector.quantize_mx(out=w_codes[g][:].bitcast(FP8X4), scales=w_sc[g][:], in_=w_bf[:])
+
+        w_bf0 = sb("w_bf0", [P, N * PACK], BF16)
+        interleave(nc.vector.tensor_copy, w_bf0[:], w_raw[0][:])
         sc_rows = sb("sc_rows", [P, S], U8)
         nc.vector.tensor_copy(sc_rows[:], scales_sb[:].indirect(offs_sb[:]))
+        quantise_w(0, w_bf0)
         for q in range(4):
             nc.sync.dma_start(
                 out=x_sc[32 * q : 32 * q + 4, :, :].rearrange("p g s -> p (g s)").bitcast(I32),
                 in_=sc_rows[32 * q : 32 * q + 32 : 4, :].bitcast(I32),
             )
         words_sb.append(load_words(1, "scales_sb"))
-        neg_coef = sb("neg_coef", [P, 2, 2], F32, tag="mem1")
-        nc.vector.tensor_scalar_mul(neg_coef[:], coef_ps[0][:, :, 0:2], -1.0)
+
         h_f32 = sb("h_f32", [P, PACK, S], F32)
-
-        for t in (2, 3):
-            decay = sb(f"decay{t}", [P, S], F32)
-            fade = sb(f"fade{t}", [P, S], F32)
+        def exp_minus(dst, t):
             nc.scalar.activation(
-                out=by_column(decay[:]), in_=gap_all, func=ACT.Relu, scale=coef[:, t - 2, 0:1], bias=coef[:, t - 2, 1:2]
+                out=by_column(dst), in_=gap_all, func=ACT.Exp, scale=neg_coef[:, t, 0:1], bias=neg_coef[:, t, 1:2]
             )
-            nc.scalar.activation(out=fade[:], in_=decay[:], func=ACT.Exp, scale=-1.0)
-            nc.vector.tensor_tensor(h_f32[:, t, :], mem_sb[t][:].indirect(slot_sb[:]), fade[:], ALU.mult)
+
+        fade = []
+        for a in range(2):
+            raw = sb(f"raw{a}", [P, S], F32)
+            exp_minus(raw[:], 2 * a)
+            fade.append(sb(f"fade{a}", [P, S], F32))
+            nc.vector.tensor_scalar_min(fade[a][:], raw[:], 1.0)
         growth = sb("growth", [P, 2, S], F32)
-        for t in range(2):
-            nc.scalar.activation(
-                out=by_column(growth[:, t, :]), in_=gap_all, func=ACT.Exp,
-                scale=neg_coef[:, t, 0:1], bias=neg_coef[:, t, 1:2],
+        for a in range(2):
+            exp_minus(growth[:, a, :], 2 * a + 1)
+        picked = [sb(f"picked{a}", [P, S], F32, tag=f"raw{a}") for a in range(2)]
+        for a in range(2):
+            nc.scalar.activation(out=picked[a][:], in_=mem_pair[a][:, U:].indirect(slot_sb[:]), func=ACT.Copy)
+            nc.vector.tensor_tensor(h_f32[:, 2 * a, :], mem_pair[a][:].indirect(slot_sb[:]), fade[a][:], ALU.mult)
+        for a in range(2):
+            nc.vector.scalar_tensor_tensor(
+                out=h_f32[:, 2 * a + 1, :], in0=growth[:, a, :], scalar=1.0, in1=picked[a][:], op0=ALU.min, op1=ALU.mult
             )
-        nc.vector.scalar_tensor_tensor(
-            out=h_f32[:, 0:2, :], in0=growth[:], scalar=1.0, in1=picked[:], op0=ALU.min, op1=ALU.mult
-        )
 
-        w_codes = [sb(f"w_codes{g}", [P, N], U32, tag=("fade3", "w_codes1", "w_codes2")[g]) for g in range(3)]
-        w_sc = [sb(f"w_sc{g}", [P, N], U8) for g in range(3)]
-
-        def quantise_w(g, copy, w_bf):
-            interleave(copy, w_bf, w_raw[g][:])
-            nc.vector.quantize_mx(out=w_codes[g][:].bitcast(FP8X4), scales=w_sc[g][:], in_=w_bf)
-
-        w_bf = sb("w_bf", [P, 2, N * PACK], BF16, tag="fade2")
-        for g in range(2):
-            quantise_w(g, nc.scalar.copy, w_bf[:, g, :])
+        w_bf1 = sb("w_bf1", [P, N * PACK], BF16, tag="fade0")
+        interleave(nc.scalar.copy, w_bf1[:], w_raw[1][:])
         h_codes = sb("h_codes", [P, S], U32)
         h_sc = sb("h_sc", [P, S], U8)
-        h_bf = [sb(f"h_bf{b}", [P, HALF * PACK], BF16, tag=("w_raw0", "h_bf1")[b]) for b in range(2)]
-        for b, copy in enumerate((nc.scalar.copy, nc.vector.tensor_copy)):
+        h_bf = [sb(f"h_bf{b}", [P, HALF * PACK], BF16) for b in range(2)]
+        for b, copy in enumerate((nc.vector.tensor_copy, nc.scalar.copy)):
             interleave(copy, h_bf[b][:], h_f32[:, :, halves[b]])
+        quantise_w(1, w_bf1, "raw0")
         for b in range(2):
             nc.vector.quantize_mx(out=h_codes[:, halves[b]].bitcast(FP8X4), scales=h_sc[:, halves[b]], in_=h_bf[b][:])
 
@@ -156,7 +156,9 @@ def tile_picked_ygrud_cand_p_kernel(
 
         x0 = sb("x_codes0", [P, S], U32, tag="h_f32")
         gather_words(0, x0)
-        quantise_w(2, nc.scalar.copy, sb("w_bf2", [P, N * PACK], BF16, tag="growth")[:])
+        w_bf2 = sb("w_bf2", [P, N * PACK], BF16, tag="growth")
+        interleave(nc.scalar.copy, w_bf2[:], w_raw[2][:])
+        quantise_w(2, w_bf2)
         x1 = sb("x_codes1", [P, S], U32, tag="w_raw2")
         gather_words(1, x1)
 

@@ -83,11 +83,13 @@ def tile_picked_ygrud_cand_p_kernel(
         gap_ps = psum.tile([P, PACK, P], F32, name="gap_ps", tag="gap_ps")
         for c in range(PACK):
             nc.tensor.transpose(gap_ps[:, c, :], gap_col[:, c : c + 1].to_broadcast([P, P]), ident[:])
-        coef_ps = psum.tile([P, PACK, P], F32, name="coef_ps")
-        for t in range(PACK):
-            nc.tensor.transpose(coef_ps[:, t, :], rows_sb[:, t:H:PACK], ident[:])
-        neg_coef = sb("neg_coef", [P, PACK, 2], F32)
-        nc.scalar.activation(out=neg_coef[:], in_=coef_ps[:, :, 0:2], func=ACT.Copy, scale=-1.0)
+        neg_coef = []
+        for a in range(2):
+            coef_ps = psum.tile([P, 2, P], F32, name=f"coef_ps{a}")
+            for t in range(2):
+                nc.tensor.transpose(coef_ps[:, t, :], rows_sb[:, 2 * a + t : H : PACK], ident[:])
+            neg_coef.append(sb(f"neg_coef{a}", [P, 2, 2], F32))
+            nc.scalar.activation(out=neg_coef[a][:], in_=coef_ps[:, :, 0:2], func=ACT.Copy, scale=-1.0)
         gap_all = gap_ps[:].rearrange("m c p -> m p c")
 
         def by_column(ap):
@@ -116,38 +118,36 @@ def tile_picked_ygrud_cand_p_kernel(
         words_sb.append(load_words(1, "scales_sb"))
 
         h_f32 = sb("h_f32", [P, PACK, S], F32)
-        def exp_minus(dst, t):
+        def exp_minus(dst, a, t):
             nc.scalar.activation(
-                out=by_column(dst), in_=gap_all, func=ACT.Exp, scale=neg_coef[:, t, 0:1], bias=neg_coef[:, t, 1:2]
+                out=by_column(dst), in_=gap_all, func=ACT.Exp, scale=neg_coef[a][:, t, 0:1], bias=neg_coef[a][:, t, 1:2]
             )
 
-        fade = []
-        for a in range(2):
-            raw = sb(f"raw{a}", [P, S], F32)
-            exp_minus(raw[:], 2 * a)
-            fade.append(sb(f"fade{a}", [P, S], F32))
-            nc.vector.tensor_scalar_min(fade[a][:], raw[:], 1.0)
         growth = sb("growth", [P, 2, S], F32)
         for a in range(2):
-            exp_minus(growth[:, a, :], 2 * a + 1)
-        picked = [sb(f"picked{a}", [P, S], F32, tag=f"raw{a}") for a in range(2)]
-        for a in range(2):
-            nc.scalar.activation(out=picked[a][:], in_=mem_pair[a][:, U:].indirect(slot_sb[:]), func=ACT.Copy)
-            nc.vector.tensor_tensor(h_f32[:, 2 * a, :], mem_pair[a][:].indirect(slot_sb[:]), fade[a][:], ALU.mult)
-        for a in range(2):
-            nc.vector.scalar_tensor_tensor(
-                out=h_f32[:, 2 * a + 1, :], in0=growth[:, a, :], scalar=1.0, in1=picked[a][:], op0=ALU.min, op1=ALU.mult
-            )
+            raw = sb(f"raw{a}", [P, S], F32)
+            exp_minus(raw[:], a, 0)
+            exp_minus(growth[:, a, :], a, 1)
+            fade = sb(f"fade{a}", [P, S], F32)
+            nc.vector.tensor_scalar_min(fade[:], raw[:], 1.0)
+            picked = sb(f"picked{a}", [P, S], F32, tag=f"raw{a}")
+            nc.scalar.activation(out=picked[:], in_=mem_pair[a][:, U:].indirect(slot_sb[:]), func=ACT.Copy)
+            nc.vector.tensor_tensor(h_f32[:, 2 * a, :], mem_pair[a][:].indirect(slot_sb[:]), fade[:], ALU.mult)
+            for cols in ([slice(0, S)], halves[::-1])[a]:
+                nc.vector.scalar_tensor_tensor(
+                    out=h_f32[:, 2 * a + 1, cols], in0=growth[:, a, cols], scalar=1.0, in1=picked[:, cols],
+                    op0=ALU.min, op1=ALU.mult,
+                )
 
-        w_bf1 = sb("w_bf1", [P, N * PACK], BF16, tag="fade0")
+        w_bf1 = sb("w_bf1", [P, N * PACK], BF16, tag="neg_coef1")
         interleave(nc.scalar.copy, w_bf1[:], w_raw[1][:])
         h_codes = sb("h_codes", [P, S], U32)
         h_sc = sb("h_sc", [P, S], U8)
         h_bf = [sb(f"h_bf{b}", [P, HALF * PACK], BF16) for b in range(2)]
+        quantise_w(1, w_bf1, "raw0")
         for b, copy in enumerate((nc.vector.tensor_copy, nc.scalar.copy)):
             interleave(copy, h_bf[b][:], h_f32[:, :, halves[b]])
-        quantise_w(1, w_bf1, "raw0")
-        for b in range(2):
+        for b in (1, 0):
             nc.vector.quantize_mx(out=h_codes[:, halves[b]].bitcast(FP8X4), scales=h_sc[:, halves[b]], in_=h_bf[b][:])
 
         def gather_words(g, codes):

@@ -68,14 +68,17 @@ def tile_picked_ygrud_cand_p_kernel(
         nc.sync.dma_start(
             out=scales_sb[0:P:4, :].bitcast(I32), in_=x_scales.rearrange("g r c -> r g c").bitcast(I32)
         )
-        for a in range(2):
-            nc.sync.dma_start(out=mem_pair[a][:], in_=mem_rows[a])
+        nc.sync.dma_start(out=mem_pair[0][:], in_=mem_rows[0])
+        for t in range(2):
+            nc.sync.dma_start(out=mem_pair[1][:, t * U : (t + 1) * U], in_=mem_rows[1][:, t * U : (t + 1) * U])
         for g in (1, 2):
             load_w(g)
 
         def load_words(g, reuse):
             words = sb(f"words{g}", [P, T], U32, tag=reuse)
-            nc.sync.dma_start(out=words[:].bitcast(I32), in_=x_words[g].rearrange("p n t -> p (n t)").bitcast(I32))
+            src = x_words[g].rearrange("p n t -> p (n t)").bitcast(I32)
+            for cols in ([slice(0, T // 2), slice(T // 2, T)], [slice(0, T)])[g]:
+                nc.sync.dma_start(out=words[:, cols].bitcast(I32), in_=src[:, cols])
             return words
 
         words_sb = [load_words(0, None)]
@@ -96,7 +99,7 @@ def tile_picked_ygrud_cand_p_kernel(
             return ap.rearrange("m (p c) -> m p c", c=PACK)
 
         halves = [slice(b * HALF, (b + 1) * HALF) for b in range(2)]
-        offs_half = [offs_sb[:, 16 * b : 16 * (b + 1)] for b in range(2)]
+        quarters = [slice(b * P, (b + 1) * P) for b in range(2)]
 
         w_codes = []
         w_sc = [sb(f"w_sc{g}", [P, N], U8) for g in range(3)]
@@ -110,7 +113,7 @@ def tile_picked_ygrud_cand_p_kernel(
         sc_rows = sb("sc_rows", [P, S], U8)
         nc.vector.tensor_copy(sc_rows[:], scales_sb[:].indirect(offs_sb[:]))
         quantise_w(0, w_bf0)
-        for q in range(4):
+        for q in (0, 2, 1, 3):
             nc.sync.dma_start(
                 out=x_sc[32 * q : 32 * q + 4, :, :].rearrange("p g s -> p (g s)").bitcast(I32),
                 in_=sc_rows[32 * q : 32 * q + 32 : 4, :].bitcast(I32),
@@ -150,34 +153,38 @@ def tile_picked_ygrud_cand_p_kernel(
         for b in (1, 0):
             nc.vector.quantize_mx(out=h_codes[:, halves[b]].bitcast(FP8X4), scales=h_sc[:, halves[b]], in_=h_bf[b][:])
 
-        def gather_words(g, codes):
-            for b in range(2):
-                nc.vector.tensor_copy(codes[:, halves[b]], words_sb[g][:].indirect(offs_half[b]))
+        def gather_words(g, codes, cuts):
+            for cols in cuts:
+                nc.vector.tensor_copy(
+                    codes[:, cols], words_sb[g][:].indirect(offs_sb[:, cols.start // 16 : cols.stop // 16])
+                )
 
         x0 = sb("x_codes0", [P, S], U32, tag="h_f32")
-        gather_words(0, x0)
+        gather_words(0, x0, halves)
         w_bf2 = sb("w_bf2", [P, N * PACK], BF16, tag="growth")
         interleave(nc.scalar.copy, w_bf2[:], w_raw[2][:])
         quantise_w(2, w_bf2)
         x1 = sb("x_codes1", [P, S], U32, tag="w_raw2")
-        gather_words(1, x1)
+        gather_words(1, x1, quarters + halves[1:])
 
-        pieces = [(0, slice(0, P)), (0, slice(P, HALF)), (1, halves[0]), (0, halves[1]), (1, halves[1])]
+        pieces = [((0,), quarters[0]), ((1,), quarters[0]), ((0, 1), quarters[1]), ((0,), halves[1]), ((1,), halves[1])]
         banks = ["acc0", "gap_ps", "acc1", "acc2", "acc3"]
         acc = [
-            psum.tile([P, cols.stop - cols.start], F32, name=f"acc_piece{i}", tag=banks[i])
-            for i, (m, cols) in enumerate(pieces)
+            psum.tile([P, len(ms), cols.stop - cols.start], F32, name=f"acc_piece{i}", tag=banks[i])
+            for i, (ms, cols) in enumerate(pieces)
         ]
+        out_rows = out.rearrange("(m p) s -> p m s", p=P)
         moving = [(0, h_codes[:], h_sc[:]), (1, x0[:], x_sc[:, 0, :]), (2, x1[:], x_sc[:, 1, :])]
         for step, (g, codes, scales) in enumerate(moving):
-            for i, (m, cols) in enumerate(pieces):
-                rows = slice(m * P, (m + 1) * P)
-                nc.tensor.matmul_mx(
-                    out=acc[i][:], lhsT=w_codes[g][:, rows].bitcast(FP8X4), lhsT_scale=w_sc[g][:, rows],
-                    rhs=codes[:, cols].bitcast(FP8X4), rhs_scale=scales[:, cols],
-                    start=(step == 0), stop=(step == 2),
-                )
+            for i, (ms, cols) in enumerate(pieces):
+                for at, m in enumerate(ms):
+                    rows = slice(m * P, (m + 1) * P)
+                    nc.tensor.matmul_mx(
+                        out=acc[i][:, at, :], lhsT=w_codes[g][:, rows].bitcast(FP8X4), lhsT_scale=w_sc[g][:, rows],
+                        rhs=codes[:, cols].bitcast(FP8X4), rhs_scale=scales[:, cols],
+                        start=(step == 0 and at == 0), stop=(step == 2 and at == len(ms) - 1),
+                    )
                 if step == 2:
-                    res = sb(f"res{i}", [P, cols.stop - cols.start], F32)
+                    res = sb(f"res{i}", [P, len(ms), cols.stop - cols.start], F32)
                     nc.scalar.activation(out=res[:], in_=acc[i][:], func=ACT.Tanh)
-                    nc.sync.dma_start(out=out[rows, cols], in_=res[:])
+                    nc.sync.dma_start(out=out_rows[:, ms[0] : ms[-1] + 1, cols], in_=res[:])

@@ -68,17 +68,14 @@ def tile_picked_ygrud_cand_p_kernel(
         nc.sync.dma_start(
             out=scales_sb[0:P:4, :].bitcast(I32), in_=x_scales.rearrange("g r c -> r g c").bitcast(I32)
         )
-        nc.sync.dma_start(out=mem_pair[0][:], in_=mem_rows[0])
-        for t in range(2):
-            nc.sync.dma_start(out=mem_pair[1][:, t * U : (t + 1) * U], in_=mem_rows[1][:, t * U : (t + 1) * U])
+        for a in range(2):
+            nc.sync.dma_start(out=mem_pair[a][:], in_=mem_rows[a])
         for g in (1, 2):
             load_w(g)
 
         def load_words(g, reuse):
             words = sb(f"words{g}", [P, T], U32, tag=reuse)
-            src = x_words[g].rearrange("p n t -> p (n t)").bitcast(I32)
-            for cols in ([slice(0, T // 2), slice(T // 2, T)], [slice(0, T)])[g]:
-                nc.sync.dma_start(out=words[:, cols].bitcast(I32), in_=src[:, cols])
+            nc.sync.dma_start(out=words[:].bitcast(I32), in_=x_words[g].rearrange("p n t -> p (n t)").bitcast(I32))
             return words
 
         words_sb = [load_words(0, None)]
@@ -99,7 +96,7 @@ def tile_picked_ygrud_cand_p_kernel(
             return ap.rearrange("m (p c) -> m p c", c=PACK)
 
         halves = [slice(b * HALF, (b + 1) * HALF) for b in range(2)]
-        quarters = [slice(b * P, (b + 1) * P) for b in range(2)]
+        quarters = [slice(b * P, (b + 1) * P) for b in range(4)]
 
         w_codes = []
         w_sc = [sb(f"w_sc{g}", [P, N], U8) for g in range(3)]
@@ -165,9 +162,9 @@ def tile_picked_ygrud_cand_p_kernel(
         interleave(nc.scalar.copy, w_bf2[:], w_raw[2][:])
         quantise_w(2, w_bf2)
         x1 = sb("x_codes1", [P, S], U32, tag="w_raw2")
-        gather_words(1, x1, quarters + halves[1:])
+        gather_words(1, x1, quarters)
 
-        pieces = [((0,), quarters[0]), ((1,), quarters[0]), ((0, 1), quarters[1]), ((0,), halves[1]), ((1,), halves[1])]
+        pieces = [((0,), quarters[0]), ((1,), quarters[0]), ((0, 1), quarters[1]), ((0, 1), quarters[2]), ((0, 1), quarters[3])]
         banks = ["acc0", "gap_ps", "acc1", "acc2", "acc3"]
         acc = [
             psum.tile([P, len(ms), cols.stop - cols.start], F32, name=f"acc_piece{i}", tag=banks[i])

@@ -19,6 +19,7 @@ ALU = mybir.AluOpType
 P = 128
 PACK = 4
 HALF = S // 2
+RATE_ROW, OFF_ROW = 16, 84
 
 
 def tile_picked_ygrud_cand_p_kernel(
@@ -63,8 +64,8 @@ def tile_picked_ygrud_cand_p_kernel(
         nc.sync.dma_start(out=gap_col[:], in_=gap[0].rearrange("(p c) -> p c", c=PACK))
         nc.sync.dma_start(offs_sb[:], offs)
         nc.sync.dma_start(slot_sb[:], slot)
-        nc.sync.dma_start(out=rows_sb[0:1, :], in_=rate.rearrange("k o -> o k"))
-        nc.sync.dma_start(out=rows_sb[1:2, :], in_=off.rearrange("k o -> o k"))
+        nc.sync.dma_start(out=rows_sb[RATE_ROW : RATE_ROW + 1, :], in_=rate.rearrange("k o -> o k"))
+        nc.sync.dma_start(out=rows_sb[OFF_ROW : OFF_ROW + 1, :], in_=off.rearrange("k o -> o k"))
         nc.sync.dma_start(
             out=scales_sb[0:P:4, :].bitcast(I32), in_=x_scales.rearrange("g r c -> r g c").bitcast(I32)
         )
@@ -89,7 +90,9 @@ def tile_picked_ygrud_cand_p_kernel(
             for t in range(2):
                 nc.tensor.transpose(coef_ps[:, t, :], rows_sb[:, 2 * a + t : H : PACK], ident[:])
             neg_coef.append(sb(f"neg_coef{a}", [P, 2, 2], F32))
-            nc.scalar.activation(out=neg_coef[a][:], in_=coef_ps[:, :, 0:2], func=ACT.Copy, scale=-1.0)
+            nc.scalar.activation(
+                out=neg_coef[a][:], in_=coef_ps[:, :, RATE_ROW : OFF_ROW + 1 : OFF_ROW - RATE_ROW], func=ACT.Copy, scale=-1.0
+            )
         gap_all = gap_ps[:].rearrange("m c p -> m p c")
 
         def by_column(ap):

@@ -31,7 +31,7 @@ def tile_picked_ygrud_cand_p_kernel(
         psum = ctx.enter_context(tc.psum_pool(name="psum", bufs=1))
 
         def sb(name, shape, dtype, tag=None):
-            return keep.tile(shape, dtype, name=name, tag=tag or name, align_bytes=64)
+            return keep.tile(shape, dtype, name=name, tag=tag or name, align_bytes=256)
 
         def interleave(copy, dst, src):
             copy(

@@ -167,8 +167,11 @@ def tile_picked_ygrud_cand_p_kernel(
         x1 = sb("x_codes1", [P, S], U32, tag="w_raw2")
         gather_words(1, x1, quarters)
 
-        pieces = [((0,), quarters[0]), ((1,), quarters[0]), ((0, 1), quarters[1]), ((0, 1), quarters[2]), ((0, 1), quarters[3])]
-        banks = ["acc0", "gap_ps", "acc1", "acc2", "acc3"]
+        pieces = [
+            ((0,), quarters[0]), ((1,), quarters[0]), ((0, 1), quarters[1]),
+            ((0,), quarters[2]), ((1,), quarters[2]), ((0,), quarters[3]), ((1,), quarters[3]),
+        ]
+        banks = ["acc0", "gap_ps", "acc1", "coef_ps0", "coef_ps1", "acc2", "acc3"]
         acc = [
             psum.tile([P, len(ms), cols.stop - cols.start], F32, name=f"acc_piece{i}", tag=banks[i])
             for i, (ms, cols) in enumerate(pieces)

@@ -61,11 +61,11 @@ def tile_picked_ygrud_cand_p_kernel(
             nc.sync.dma_start(out=w_raw[g][:], in_=w_src[g].rearrange("(p t) n -> p t n", t=PACK))
 
         load_w(0)
+        nc.sync.dma_start(out=rows_sb[RATE_ROW : RATE_ROW + 1, :], in_=rate.rearrange("k o -> o k"))
+        nc.sync.dma_start(out=rows_sb[OFF_ROW : OFF_ROW + 1, :], in_=off.rearrange("k o -> o k"))
         nc.sync.dma_start(out=gap_col[:], in_=gap[0].rearrange("(p c) -> p c", c=PACK))
         nc.sync.dma_start(offs_sb[:], offs)
         nc.sync.dma_start(slot_sb[:], slot)
-        nc.sync.dma_start(out=rows_sb[RATE_ROW : RATE_ROW + 1, :], in_=rate.rearrange("k o -> o k"))
-        nc.sync.dma_start(out=rows_sb[OFF_ROW : OFF_ROW + 1, :], in_=off.rearrange("k o -> o k"))
         nc.sync.dma_start(
             out=scales_sb[0:P:4, :].bitcast(I32), in_=x_scales.rearrange("g r c -> r g c").bitcast(I32)
         )
@@ -81,18 +81,21 @@ def tile_picked_ygrud_cand_p_kernel(
 
         words_sb = [load_words(0, None)]
 
-        gap_ps = psum.tile([P, PACK, P], F32, name="gap_ps", tag="gap_ps")
-        for c in range(PACK):
-            nc.tensor.transpose(gap_ps[:, c, :], gap_col[:, c : c + 1].to_broadcast([P, P]), ident[:])
         neg_coef = []
-        for a in range(2):
-            coef_ps = psum.tile([P, 2, P], F32, name=f"coef_ps{a}")
+
+        def turn_coefficients(a):
+            coef_ps = psum.tile([P, 2, P], F32, name=f"coef_ps{a}", tag="coef_ps")
             for t in range(2):
                 nc.tensor.transpose(coef_ps[:, t, :], rows_sb[:, 2 * a + t : H : PACK], ident[:])
             neg_coef.append(sb(f"neg_coef{a}", [P, 2, 2], F32))
-            nc.scalar.activation(
-                out=neg_coef[a][:], in_=coef_ps[:, :, RATE_ROW : OFF_ROW + 1 : OFF_ROW - RATE_ROW], func=ACT.Copy, scale=-1.0
-            )
+            negate = (nc.scalar.mul, nc.vector.tensor_scalar_mul)[a]
+            negate(neg_coef[a][:], coef_ps[:, :, RATE_ROW : OFF_ROW + 1 : OFF_ROW - RATE_ROW], -1.0)
+
+        turn_coefficients(0)
+        gap_ps = psum.tile([P, PACK, P], F32, name="gap_ps", tag="gap_ps")
+        for c in range(PACK):
+            nc.tensor.transpose(gap_ps[:, c, :], gap_col[:, c : c + 1].to_broadcast([P, P]), ident[:])
+        turn_coefficients(1)
         gap_all = gap_ps[:].rearrange("m c p -> m p c")
 
         def by_column(ap):
@@ -160,7 +163,7 @@ def tile_picked_ygrud_cand_p_kernel(
                 )
 
         x0 = sb("x_codes0", [P, S], U32, tag="h_f32")
-        gather_words(0, x0, halves)
+        gather_words(0, x0, [slice(0, S)])
         w_bf2 = sb("w_bf2", [P, N * PACK], BF16, tag="growth")
         interleave(nc.scalar.copy, w_bf2[:], w_raw[2][:])
         quantise_w(2, w_bf2)
@@ -171,7 +174,7 @@ def tile_picked_ygrud_cand_p_kernel(
             ((0,), quarters[0]), ((1,), quarters[0]), ((0, 1), quarters[1]),
             ((0,), quarters[2]), ((1,), quarters[2]), ((0,), quarters[3]), ((1,), quarters[3]),
         ]
-        banks = ["acc0", "gap_ps", "acc1", "coef_ps0", "coef_ps1", "acc2", "acc3"]
+        banks = ["acc0", "gap_ps", "acc1", "coef_ps", "acc2", "acc3", "acc4"]
         acc = [
             psum.tile([P, len(ms), cols.stop - cols.start], F32, name=f"acc_piece{i}", tag=banks[i])
             for i, (ms, cols) in enumerate(pieces)

from contextlib import ExitStack

import concourse.mybir as mybir
from concourse.masks import make_identity

K, T, S, H, N, U = 1024, 2048, 512, 512, 256, 1024
FLOPS = 2 * (K + H) * N * S

F32 = mybir.dt.float32
BF16 = mybir.dt.bfloat16
I32 = mybir.dt.int32
U32 = mybir.dt.uint32
U16 = mybir.dt.uint16
U8 = mybir.dt.uint8
FP8X4 = mybir.dt.float8_e4m3fn_x4
ACT = mybir.ActivationFunctionType
ALU = mybir.AluOpType

P = 128
PACK = 4
HALF = S // 2
RATE_ROW, OFF_ROW = 16, 84


def tile_picked_ygrud_cand_p_kernel(
    tc, x_words, x_scales, mem, gap, rate, off, w1, rr, offs, slot, out
):
    nc = tc.nc
    with ExitStack() as ctx:
        keep = ctx.enter_context(tc.tile_pool(name="keep", bufs=1))
        psum = ctx.enter_context(tc.psum_pool(name="psum", bufs=1))

        def sb(name, shape, dtype, tag=None):
            return keep.tile(shape, dtype, name=name, tag=tag or name, align_bytes=256)

        def interleave(copy, dst, src):
            copy(
                out=dst.rearrange("p (c i t) -> p c t i", i=4, t=PACK),
                in_=src.rearrange("p t (c i) -> p c t i", i=4),
            )

        offs_sb = sb("offs_sb", [P, S // 16], U16)
        slot_sb = sb("slot_sb", [P, S // 16], U16)
        gap_col = sb("gap_col", [P, PACK], F32)
        rows_sb = sb("rows_sb", [P, H], F32)
        mem_pair = [sb(f"mem{a}", [P, 2 * U], F32) for a in range(2)]
        scales_sb = sb("scales_sb", [P, T], U8)
        w_raw = [sb(f"w_raw{g}", [P, PACK, N], F32) for g in range(3)]
        w_src = [rr, w1[0:512, :], w1[512:1024, :]]
        x_sc = sb("x_sc", [P, 2, S], U8)
        ident = sb("ident", [P, P], F32)

        nc.gpsimd.memset(rows_sb[:], 0.0)
        nc.vector.memset(scales_sb[:].bitcast(I32), 0)
        nc.vector.memset(x_sc[:].rearrange("p g s -> p (g s)").bitcast(I32), 0)
        make_identity(nc, ident[:])

        mem_rows = mem.rearrange("(p a t) u -> a p (t u)", a=2, t=2)

        def load_w(g):
            nc.sync.dma_start(out=w_raw[g][:], in_=w_src[g].rearrange("(p t) n -> p t n", t=PACK))

        load_w(0)
        nc.sync.dma_start(out=rows_sb[RATE_ROW : RATE_ROW + 1, :], in_=rate.rearrange("k o -> o k"))
        nc.sync.dma_start(out=rows_sb[OFF_ROW : OFF_ROW + 1, :], in_=off.rearrange("k o -> o k"))
        nc.sync.dma_start(out=gap_col[:], in_=gap[0].rearrange("(p c) -> p c", c=PACK))
        nc.sync.dma_start(offs_sb[:], offs)
        nc.sync.dma_start(slot_sb[:], slot)
        nc.sync.dma_start(
            out=scales_sb[0:P:4, :].bitcast(I32), in_=x_scales.rearrange("g r c -> r g c").bitcast(I32)
        )
        for a in range(2):
            nc.sync.dma_start(out=mem_pair[a][:], in_=mem_rows[a])
        for g in (1, 2):
            load_w(g)

        def load_words(g, reuse):
            words = sb(f"words{g}", [P, T], U32, tag=reuse)
            nc.sync.dma_start(out=words[:].bitcast(I32), in_=x_words[g].rearrange("p n t -> p (n t)").bitcast(I32))
            return words

        words_sb = [load_words(0, None)]

        neg_coef = []

        def turn_coefficients(a):
            coef_ps = psum.tile([P, 2, P], F32, name=f"coef_ps{a}", tag="coef_ps")
            for t in range(2):
                nc.tensor.transpose(coef_ps[:, t, :], rows_sb[:, 2 * a + t : H : PACK], ident[:])
            neg_coef.append(sb(f"neg_coef{a}", [P, 2, 2], F32))
            negate = (nc.scalar.mul, nc.vector.tensor_scalar_mul)[a]
            negate(neg_coef[a][:], coef_ps[:, :, RATE_ROW : OFF_ROW + 1 : OFF_ROW - RATE_ROW], -1.0)

        turn_coefficients(0)
        gap_ps = psum.tile([P, PACK, P], F32, name="gap_ps", tag="gap_ps")
        for c in range(PACK):
            nc.tensor.transpose(gap_ps[:, c, :], gap_col[:, c : c + 1].to_broadcast([P, P]), ident[:])
        turn_coefficients(1)
        gap_all = gap_ps[:].rearrange("m c p -> m p c")

        def by_column(ap):
            return ap.rearrange("m (p c) -> m p c", c=PACK)

        halves = [slice(b * HALF, (b + 1) * HALF) for b in range(2)]
        quarters = [slice(b * P, (b + 1) * P) for b in range(4)]

        w_codes = []
        w_sc = [sb(f"w_sc{g}", [P, N], U8) for g in range(3)]

        def quantise_w(g, w_bf, reuse=None):
            w_codes.append(sb(f"w_codes{g}", [P, N], U32, tag=reuse))
            nc.vector.quantize_mx(out=w_codes[g][:].bitcast(FP8X4), scales=w_sc[g][:], in_=w_bf[:])

        w_bf0 = sb("w_bf0", [P, N * PACK], BF16)
        interleave(nc.vector.tensor_copy, w_bf0[:], w_raw[0][:])
        sc_rows = sb("sc_rows", [P, S], U8)
        nc.vector.tensor_copy(sc_rows[:], scales_sb[:].indirect(offs_sb[:]))
        quantise_w(0, w_bf0)
        for q in (0, 2, 1, 3):
            nc.sync.dma_start(
                out=x_sc[32 * q : 32 * q + 4, :, :].rearrange("p g s -> p (g s)").bitcast(I32),
                in_=sc_rows[32 * q : 32 * q + 32 : 4, :].bitcast(I32),
            )
        words_sb.append(load_words(1, "scales_sb"))

        h_f32 = sb("h_f32", [P, PACK, S], F32)
        def exp_minus(dst, a, t):
            nc.scalar.activation(
                out=by_column(dst), in_=gap_all, func=ACT.Exp, scale=neg_coef[a][:, t, 0:1], bias=neg_coef[a][:, t, 1:2]
            )

        growth = sb("growth", [P, 2, S], F32)
        for a in range(2):
            raw = sb(f"raw{a}", [P, S], F32)
            exp_minus(raw[:], a, 0)
            exp_minus(growth[:, a, :], a, 1)
            fade = sb(f"fade{a}", [P, S], F32)
            nc.vector.tensor_scalar_min(fade[:], raw[:], 1.0)
            picked = sb(f"picked{a}", [P, S], F32, tag=f"raw{a}")
            nc.scalar.activation(out=picked[:], in_=mem_pair[a][:, U:].indirect(slot_sb[:]), func=ACT.Copy)
            nc.vector.tensor_tensor(h_f32[:, 2 * a, :], mem_pair[a][:].indirect(slot_sb[:]), fade[:], ALU.mult)
            for cols in ([slice(0, S)], halves[::-1])[a]:
                nc.vector.scalar_tensor_tensor(
                    out=h_f32[:, 2 * a + 1, cols], in0=growth[:, a, cols], scalar=1.0, in1=picked[:, cols],
                    op0=ALU.min, op1=ALU.mult,
                )

        w_bf1 = sb("w_bf1", [P, N * PACK], BF16, tag="neg_coef1")
        interleave(nc.scalar.copy, w_bf1[:], w_raw[1][:])
        h_codes = sb("h_codes", [P, S], U32)
        h_sc = sb("h_sc", [P, S], U8)
        h_bf = [sb(f"h_bf{b}", [P, HALF * PACK], BF16) for b in range(2)]
        quantise_w(1, w_bf1, "raw0")
        for b, copy in enumerate((nc.vector.tensor_copy, nc.scalar.copy)):
            interleave(copy, h_bf[b][:], h_f32[:, :, halves[b]])
        for b in (1, 0):
            nc.vector.quantize_mx(out=h_codes[:, halves[b]].bitcast(FP8X4), scales=h_sc[:, halves[b]], in_=h_bf[b][:])

        def gather_words(g, codes, cuts):
            for cols in cuts:
                nc.vector.tensor_copy(
                    codes[:, cols], words_sb[g][:].indirect(offs_sb[:, cols.start // 16 : cols.stop // 16])
                )

        x0 = sb("x_codes0", [P, S], U32, tag="h_f32")
        gather_words(0, x0, [slice(0, S)])
        w_bf2 = sb("w_bf2", [P, N * PACK], BF16, tag="growth")
        interleave(nc.scalar.copy, w_bf2[:], w_raw[2][:])
        quantise_w(2, w_bf2)
        x1 = sb("x_codes1", [P, S], U32, tag="w_raw2")
        gather_words(1, x1, quarters)

        pieces = [
            ((0,), quarters[0]), ((1,), quarters[0]), ((0, 1), quarters[1]),
            ((0,), quarters[2]), ((1,), quarters[2]), ((0,), quarters[3]), ((1,), quarters[3]),
        ]
        banks = ["acc0", "gap_ps", "acc1", "coef_ps", "acc2", "acc3", "acc4"]
        acc = [
            psum.tile([P, len(ms), cols.stop - cols.start], F32, name=f"acc_piece{i}", tag=banks[i])
            for i, (ms, cols) in enumerate(pieces)
        ]
        out_rows = out.rearrange("(m p) s -> p m s", p=P)
        moving = [(0, h_codes[:], h_sc[:]), (1, x0[:], x_sc[:, 0, :]), (2, x1[:], x_sc[:, 1, :])]
        for step, (g, codes, scales) in enumerate(moving):
            for i, (ms, cols) in enumerate(pieces):
                for at, m in enumerate(ms):
                    rows = slice(m * P, (m + 1) * P)
                    nc.tensor.matmul_mx(
                        out=acc[i][:, at, :], lhsT=w_codes[g][:, rows].bitcast(FP8X4), lhsT_scale=w_sc[g][:, rows],
                        rhs=codes[:, cols].bitcast(FP8X4), rhs_scale=scales[:, cols],
                        start=(step == 0 and at == 0), stop=(step == 2 and at == len(ms) - 1),
                    )
                if step == 2:
                    res = sb(f"res{i}", [P, len(ms), cols.stop - cols.start], F32)
                    nc.scalar.activation(out=res[:], in_=acc[i][:], func=ACT.Tanh)
                    nc.sync.dma_start(out=out_rows[:, ms[0] : ms[-1] + 1, cols], in_=res[:])
